import numpy as np, ml_dtypes
CORES = [242,247,114,119]
N = 4
BF = ml_dtypes.bfloat16
def gentries(a):
    return np.ascontiguousarray(a.reshape(8, 16, -1).transpose(0, 2, 1)).reshape(8, -1)
def gtable(e):
    e = np.asarray(e); return np.ascontiguousarray(e.reshape(8, -1, 16).transpose(0, 2, 1)).reshape(128, -1).astype(np.int32)
def f(rng, *shape):
    return (rng.standard_normal(shape, dtype=np.float32) * np.exp2(rng.integers(-2, 3, shape[:-1] + (1,)))).astype(BF)
def wide(rng, *shape):
    v = f(rng, *shape).astype(np.float32); k = shape[:-2] + (1, shape[-1])
    return (v * np.exp2(rng.integers(-6, 7, k)) * (rng.random(k) > 0.0625)).astype(BF)
W, R, TK, A = 1280, 576, 5, 80
X = np.arange(16)[:, None]
def cols(rng, lo, hi, lead, m=16):
    sh = rng.integers(lo, hi, lead + (1, W)); z = np.zeros(lead + (1, W), np.int64)
    c = np.sort((rng.integers(0, 257, lead + (m - 1, W)) >> sh) << sh, axis=-2)
    v = np.diff(np.concatenate([z, c, z + 256], axis=-2), axis=-2)
    return np.take_along_axis(v, np.argsort(rng.random(v.shape), axis=-2), -2)
def parts(rng, lo=0, hi=8):
    P = cols(rng, lo, hi, (8,)); a = cols(rng, lo, hi, (N, 8)); m = (P + a) >> 1
    m = m + (256 - np.add.reduce(m, axis=-2, keepdims=True)) * (X == rng.integers(0, 16, (N, 8, 1, W)))
    return {"P": P, "Q": np.where(rng.random((N, 8, 1, W)) < 0.5, m, a), "E": rng.integers(0, A, (8, 16, W)), "V": np.clip(f(rng, 128, W).astype(np.float32), -2, 2),
            "n": rng.integers(0, W, (N, 8, R)), "s": np.argsort(rng.random((N, 8, TK, W)), axis=-1)[..., :R], "d": rng.integers(0, 256, (N, 8, TK, 2, R)), "a": rng.integers(0, 128, (N, 8, TK, 3, R))}
def pack(v):
    def small(a): return np.ascontiguousarray(a).astype(np.float32).astype(BF)
    def alike(a): return small(np.stack([np.reshape(a, (128, W))] * N))
    return {"pt": alike(v["P"]), "qd": small(v["Q"].reshape(N, 128, W)), "nx": alike(v["E"]), "vf": alike(v["V"]), "n0": np.stack([gtable(a) for a in v["n"]]),
            "spot": np.stack([gtable(a.reshape(8, -1)) for a in v["s"]]), "ud": small(v["d"].reshape(N, 8, 2 * TK * R)), "ua": small(v["a"].reshape(N, 8, 3 * TK * R))}
def setup_inputs(rng):
    return pack(parts(rng))
def setup_inputs_spread(rng):
    v = parts(rng, 0, 9); v["V"] = np.clip(wide(rng, 128, W).astype(np.float32) * 0.5, -2, 2)
    r = rng.random((N, 8, R)); v["n"] = (W * r * r * r).astype(np.int64); r = rng.random((8, 16, W)); v["E"] = (A * r * r).astype(np.int64)
    r = rng.random(v["d"].shape); v["d"] = (256 * np.where(rng.random((N, 8, TK, 2, 1)) < 0.5, r * r, 1 - r * r * r)).astype(np.int64) & 255
    r = rng.random(v["a"].shape); v["a"] = (128 * np.where(rng.random((N, 8, TK, 3, 1)) < 0.5, r * r, 1 - r * r * r)).astype(np.int64) & 127
    return pack(v)
def two(rng, lead):
    a = rng.integers(0, 16, lead + (1, W)); b = (a + rng.integers(1, 16, lead + (1, W))) & 15; k = rng.choice(np.array([256, 256, 256, 255, 128, 1]), lead + (1, W))
    return k * (X == a) + (256 - k) * (X == b)
def setup_inputs_ends(rng):
    v = parts(rng); v["P"] = two(rng, (8,)); v["Q"] = two(rng, (N, 8)); x = np.arange(16)
    v["P"][7, :, W - 1] = 256 * (x == 15); v["Q"][:, 7, :, W - 1] = 256 * (x == 0); v["P"][2, :, 0] = 256 * (x == 14); v["Q"][:, 2, :, 0] = 256 * (x == 1)
    v["E"] = (A - 1) * rng.integers(0, 2, (8, 16, W)); v["V"] = 4.0 * rng.integers(0, 2, (128, W)) - 2.0
    v["n"] = (W - 1) * rng.integers(0, 2, (N, 8, R)); v["n"][:, :, R - 1] = W - 1; v["n"][:, :, 0] = 0
    ends = np.concatenate([np.arange(R // 2), np.arange(W - R // 2, W)]); v["s"] = ends[np.argsort(rng.random((N, 8, TK, R)), axis=-1)]
    v["d"] = 255 * rng.integers(0, 2, v["d"].shape); v["a"] = 127 * rng.integers(0, 2, v["a"].shape)
    return pack(v)
def odd(v, par):
    return np.where((X & 1) == par, np.repeat(v, 2, axis=-2), 0)
def setup_inputs_corners(rng):
    v = parts(rng); par = rng.integers(0, 2, (8, 1, W)); D = odd(cols(rng, 0, 8, (N, 8), 8), 1 - par)
    y = np.arange(8)[:, None]; i = rng.integers(0, 8, (8, 1, W)); j = (i + rng.integers(1, 8, (8, 1, W))) & 7; b = rng.integers(1, 65, (8, 1, W))
    P = odd(np.where(rng.random((8, 1, W)) < 0.4, (256 - b) * (y == i) + b * (y == j), cols(rng, 0, 8, (8,), 8)), par)
    top = (X == np.argmax(P, axis=-2)[..., None, :]) * 1; big = (X == np.argmax(D, axis=-2)[..., None, :]) * 1
    rest = P * (1 - top); nxt = (X == np.argmax(rest, axis=-2)[..., None, :]) * 1
    D = D + rng.integers(0, 2, (N, 8, 1, W)) * (top - big); edge = (X == np.where(par == 1, 0, 15)) * 1
    k = rng.integers(1, 4, (N, 8, 1, W)); both = ((k >= 2) & (np.max(rest, axis=-2, keepdims=True) >= 1)) * 1
    near = P + k * (edge - top) + both * (top - nxt)
    kind = np.array([0, 1, 1, 2, 3, 2, 0, 3])[(np.arange(N)[:, None] + np.arange(8)) & 7][:, :, None, None]
    v["P"] = P; v["Q"] = np.where(kind == 0, P, np.where(kind == 1, D, np.where(kind == 2, near, v["Q"])))
    v["d"] = np.where(rng.random(v["d"].shape) < 0.7, rng.choice(np.array([0, 1, 2, 3, 252, 253, 254, 255]), v["d"].shape), v["d"])
    v["a"] = np.where(rng.random(v["a"].shape) < 0.7, rng.choice(np.array([0, 1, 126, 127]), v["a"].shape), v["a"])
    v["n"] = np.where(rng.random(v["n"].shape) < 0.2, rng.choice(np.array([0, W - 1]), v["n"].shape), v["n"])
    v["E"] = np.where(rng.random(v["E"].shape) < 0.2, rng.choice(np.array([0, A - 1]), v["E"].shape), v["E"])
    return pack(v)
def setup_inputs_ties(rng):
    v = parts(rng); P = cols(rng, 4, 8, (8,)); Q = np.where(rng.random((N, 8, 1, W)) < 0.33, P, cols(rng, 4, 8, (N, 8)))
    o = np.argsort(rng.random((8, 16, W)), axis=-2); k = rng.choice(np.array([41, 47, 55, 61]), (8, 1, W)); i = rng.integers(0, 4, (N, 8, 1, W)); own = rng.random((8, 1, W)) < 0.4
    one = 256 * (o == 4); half = 128 * ((o == i) | (o == ((i + 1) & 3)))
    v["P"] = np.where(own, np.where(o < 4, k, (256 - 4 * k) * (o == 4)), P)
    v["Q"] = np.where(own, np.where(rng.random((N, 8, 1, W)) < 0.5, one, half), Q)
    v["d"] = np.clip(16 * rng.integers(0, 17, v["d"].shape) - rng.integers(0, 2, v["d"].shape), 0, 255)
    v["a"] = rng.choice(np.array([0, 16, 31, 32, 33, 48, 63, 64, 65, 80, 96, 112, 127]), v["a"].shape)
    v["a"][:, :, :, 1] = np.where(rng.random((N, 8, TK, R)) < 0.3, 64, v["a"][:, :, :, 1])
    return pack(v)
def setup_inputs_alike(rng):
    v = parts(rng); c = rng.integers(0, W - 1, (N, 8, 1)); v["n"] = c + np.zeros((N, 8, R), np.int64); v["n"][:, 1::2, R - 1] += 1
    b = rng.integers(0, A - 3, (8, 1, 1)); v["E"] = b + 3 * rng.integers(0, 2, (8, 16, W))
    k = rng.integers(0, W, 64)[rng.integers(0, 64, W)]; v["P"] = v["P"][:, :, k]
    return pack(v)
def check_ranges(d):
    bad = []
    for k, lo, hi in (("pt", 0, 256), ("qd", 0, 256), ("nx", 0, A - 1), ("vf", -2, 2), ("n0", 0, W - 1), ("spot", 0, W - 1), ("ud", 0, 255), ("ua", 0, 127)):
        a = np.asarray(d[k]).astype(np.float64)
        if not (np.min(a) >= lo and np.max(a) <= hi): bad.append("range of " + k)
        if k != "vf" and not np.all(a == np.floor(a)): bad.append("whole numbers of " + k)
        if k in ("pt", "nx", "vf") and not np.all(a == a[:1]): bad.append(k + " alike on all ranks")
        if k in ("pt", "qd") and not np.all(np.add.reduce(a.reshape(N, 8, 16, W), axis=2) == 256): bad.append("sums of " + k)
    s = np.sort(np.stack([gentries(np.asarray(a)) for a in d["spot"]]).reshape(N, 8, TK, R), axis=-1)
    if np.any(s[..., 1:] == s[..., :-1]): bad.append("repeated places in spot")
    return bad
def pick(tab, n):
    return np.take_along_axis(tab, n[:, :, None, :], 3)
def at(v, x):
    return np.take_along_axis(v, x[:, :, None, :], 2)[:, :, 0]
def first(m):
    return np.argmax(m, axis=2)
def teach(Q, rej, pl, p):
    for r in range(N):
        for g in range(8):
            k = rej[r, g]; Q[r, g][:, pl[r, g, k]] = p[r, g][:, k]
def reference(pt, qd, nx, vf, n0, spot, ud, ua):
    def ints(a): return a.astype(np.float32).astype(np.int64)
    P = ints(pt).reshape(N, 8, 16, W); Q = ints(qd).reshape(N, 8, 16, W); E = ints(nx).reshape(N, 8, 16, W); v = vf.astype(np.float64).reshape(N, 8, 16, W)
    n = np.stack([gentries(a) for a in n0]).astype(np.int64); pl = np.stack([gentries(a) for a in spot]).astype(np.int64).reshape(N, 8, TK, R)
    u = ints(ud).reshape(N, 8, TK, 2, R); w = ints(ua).reshape(N, 8, TK, 3, R); h = np.zeros((N, 8, 16, R)); seen = []
    for t in range(TK):
        p = pick(P, n); q = pick(Q, n)
        x = first(np.add.accumulate(q, axis=2) > u[:, :, t, 0][:, :, None])
        rej = w[:, :, t, 0] * at(q, x) >= 128 * at(p, x)
        p1 = np.maximum(p - q, 0)
        teach(Q, rej, pl[:, :, t], p)
        n, x, rej, p1, h = [np.roll(a, 1, axis=0) for a in (n, x, rej, p1, h)]
        s = np.add.reduce(p1, axis=2); p = pick(P, n); q = pick(Q, n)
        y = first(np.add.accumulate(q, axis=2) > u[:, :, t, 1][:, :, None])
        again = rej & (w[:, :, t, 1] * at(q, y) * s >= 32768 * at(p1, y))
        c = np.add.accumulate(np.maximum(256 * p1 - s[:, :, None] * q, 0), axis=2)
        z = first(128 * c > w[:, :, t, 2][:, :, None] * c[:, :, 15:])
        x = np.where(again, z, np.where(rej, y, x))
        if t < TK - 1: teach(Q, again, pl[:, :, t], p)
        row = np.concatenate([x[:, :1], (x[:, 1:] + x[:, :-1]) & 15], axis=1)
        n = 16 * at(pick(E, n), row) + x
        h = np.tanh(h + pick(v, n)); seen.append(n)
    yn = np.stack(seen, axis=2).reshape(N, 8, TK * R)
    return {"yh": h.reshape(N, 128, R).astype(np.float32), "yn": np.stack([gtable(a) for a in yn]).astype(np.float32)}

def check_inputs(d):
    bad = list(check_ranges(d))
    if not bad:
        for name, y in reference(**d).items():
            for q in range(N):
                v = np.abs(np.asarray(y[q], np.float64)); s = np.sqrt(np.mean(v * v))
                if v.max() > 3 * s or s < 2.0 ** -3: bad.append('%s of rank %d is uneven or too small' % (name, q))
    return bad

@@ -1,0 +1,403 @@
+from concourse.mybir import AluOpType as ALU, ActivationFunctionType as ACT
+
+W, R, TK, C = 1280, 576, 5, 36
+H = R // 2
+RW = 2 * C + R
+LS = 40
+
+SCRATCH = {
+    "Q": ("sbuf", [128, 3 * W], "bfloat16"), "P": ("sbuf", [128, W], "bfloat16"),
+    "E": ("sbuf", [128, W], "bfloat16"), "F": ("sbuf", [128, W], "bfloat16"),
+    "UD": ("sbuf", [128, 2 * TK * R], "bfloat16"), "UA": ("sbuf", [128, 3 * TK * R], "bfloat16"),
+    "n0i": ("sbuf", [128, C], "int32"), "n0f": ("sbuf", [128, C], "float32"), "spi": ("sbuf", [128, TK * C], "int32"),
+    "sp1": ("sbuf", [128, TK * C], "float32"), "sp2": ("sbuf", [128, TK * C], "float32"),
+    "RS": ("sbuf", [128, (TK + 1) * RW], "bfloat16"), "RI": ("sbuf", [128, TK * RW], "bfloat16"),
+    "NL": ("sbuf", [128, (TK + 1) * LS], "uint16"), "NI": ("sbuf", [128, TK * LS], "uint16"),
+    "HI": ("sbuf", [128, 2 * LS], "uint16"),
+    "MS": ("sbuf", [128, TK * 2 * C], "bfloat16"), "MI": ("sbuf", [128, TK * 2 * C], "bfloat16"),
+    "VL": ("sbuf", [128, LS], "bfloat16"), "OF1": ("sbuf", [128, LS], "uint16"), "OF2": ("sbuf", [128, LS], "uint16"),
+    "SG": ("sbuf", [128, LS], "uint16"), "YN": ("sbuf", [128, TK * C], "float32"),
+    "ji": ("sbuf", [128, 144], "bfloat16"), "pi": ("sbuf", [128, 4], "int32"), "col": ("sbuf", [128, 16], "bfloat16"),
+    "OH": ("sbuf", [128, 32], "bfloat16"), "ON": ("sbuf", [128, 32], "bfloat16"), "t4": ("sbuf", [128, 32], "bfloat16"),
+}
+for _n in ("p1", "q1", "s1", "fo1", "p2", "q2", "s2", "fo2", "sv", "ec", "eo", "og", "sb"):
+    SCRATCH[_n] = ("sbuf", [128, R], "bfloat16")
+for _n in ("cq", "sq", "wr", "wp", "ew", "dq", "hh", "hx"):
+    SCRATCH[_n] = ("sbuf", [128, R], "float32")
+for _n in ("mL", "mI", "mO1", "mO2", "mP", "mM", "mB", "mF", "mH", "mG", "mS", "sN", "sC", "sE",
+           "um", "gm", "blk", "t0", "t1", "t2", "t3"):
+    SCRATCH[_n] = ("sbuf", [128, 128], "bfloat16")
+for _n in ("fL", "fB", "fI"):
+    SCRATCH[_n] = ("sbuf", [128, 128], "float32")
+for _n in ("wV", "wW", "wX", "wU"):
+    SCRATCH[_n] = ("sbuf", [128, 144], "bfloat16")
+for _i in range(8):
+    SCRATCH["b%d" % _i] = ("psum", [128, 512], "float32")
+
+LOADS = ["n0", "qd", "pt", "ud", "ue", "ua", "ub", "spot", "nx", "vf"]
+SEMAPHORES = (["cV", "cS", "cP", "cG", "sent", "stored", "ah0", "ah1", "hd2", "hd3"] + ["ld_" + n for n in LOADS]
+              + ["%s%d" % (k, t) for t in range(TK) for k in ("aa", "ab", "am")])
+
+X2CUT = [0, 36, 36, 36]
+TAIL = [18, 28, 36]
+FB = "A"
+FD = ""
+FIRST = """aA cA aB cB gqA gqB LqA LqB sgA cqA gpA dlA rlA IpA pmA txA gpB dlB IpB spc pA spd late""".split()
+ORDER = """fA sgB c1a rlB pmB cqB th fB c1b pB ofA cd1 txB cvB x1A cd2 bB msg ofB dA SA x1B ScA nm bA nc dB qqA sn o2p eA IrA L2A SB
+sqA wrA IrB qqB sqB I2A dqA L2B wrB s2A rwA p2A s2B rwB eB LwA dqB f2A g2B I2B p2B f2B ewA g2A LwB o2c ewB OwA kB ecg ovA OwB ovB svA
+vpA cvvA kA tkB of2 svB hg x2a vmxA +aA vpB sgmA cvvB sgcA +aB eoA vmxB sgmB sgcB cveA eoB nlA hiA hd tkA +gqA cveB nlB ynA +gpA +LqA
+hiB +sgA +dlA +IpA +rlA loA loB ynB +txA +cA +gpB +pmA +cB +gqB +pA +LqB +dlB +IpB +cqA""".split()
+
+
+def emit(g, T, ops, final):
+    queue = {"V": g.vector, "S": g.scalar, "P": g.tensor, "G": g, "Y": g.sync}
+    last_w, readers, last_b, deps = {}, {}, {}, []
+    for i, (e, fn, rd, wr, bk, done) in enumerate(ops):
+        d = set()
+        for k in rd:
+            d.add(last_w[k])
+        for k in wr:
+            d.update(readers.get(k, []) + ([last_w[k]] if k in last_w else []))
+        for k in bk:
+            if k in last_b and ops[last_b[k]][0] != e: d.add(last_b[k])
+        d.discard(i)
+        deps.append(d)
+        for k in rd: readers.setdefault(k, []).append(i)
+        for k in wr:
+            last_w[k] = i
+            readers[k] = []
+        for k in bk: last_b[k] = i
+    pos, cnt = [], {}
+    for e, fn, rd, wr, bk, done in ops:
+        cnt[e] = cnt.get(e, 0) + 1
+        pos.append(cnt[e])
+    know = {e: {} for e in list(queue) + ["X"]}
+    clock, waits, needed = [], [], set()
+    for i, (e, fn, rd, wr, bk, done) in enumerate(ops):
+        w = []
+        for j in sorted(deps[i], reverse=True):
+            key = ops[j][5][0] if ops[j][5] is not None else ops[j][0]
+            if know[e].get(key, 0) >= pos[j]: continue
+            w.append(j)
+            needed.add(j)
+            for k, v in clock[j].items():
+                if know[e].get(k, 0) < v: know[e][k] = v
+        waits.append(w)
+        c = dict(know[e])
+        c[done[0] if done is not None else e] = pos[i]
+        clock.append(c)
+    val, n, seen = {}, {}, {}
+    for i, (e, fn, rd, wr, bk, done) in enumerate(ops):
+        for j in waits[i]:
+            s, v = ops[j][5] if ops[j][5] is not None else ("c" + ops[j][0], val[j])
+            queue[e].wait_ge(T.sem[s], v)
+            seen[s] = max(seen.get(s, 0), v)
+        if fn is None: continue
+        ins = fn()
+        if done is not None:
+            if ins is not None: ins.then_inc(T.sem[done[0]], 16)
+        elif i in needed:
+            n[e] = n.get(e, 0) + 1
+            val[i] = n[e]
+            ins.then_inc(T.sem["c" + e], 1)
+    for s, v in final:
+        if seen.get(s, 0) < v: g.wait_ge(T.sem[s], v)
+
+
+def rank_program(g, core, T, topo):
+    rank = T.rank_of(core)
+    if rank is None:
+        return
+    N = len(T.cores)
+    nxt, prv, opp = T.cores[(rank + 1) % N], T.cores[(rank - 1) % N], T.cores[(rank + 2) % N]
+    ops, final, sent = [], [], [0]
+    V, S, PE = g.vector, g.scalar, g.tensor
+
+    def op(e, fn, rd, wr, bk=(), done=None):
+        ops.append((e, fn, list(rd), list(wr), list(bk), done))
+
+    def arrives(sem, count, keys):
+        op("X", None, [], keys, done=(sem, count))
+        final.append((sem, count))
+
+    def hs(h): return slice(h * H, (h + 1) * H)
+    def lst(buf, k, a=0, b=C): return buf[:, k * LS + a:k * LS + b]
+    def bank(i): return T["b%d" % i]
+    def bh(i): return bank(i)[:, 0:H]
+    def bl(i, n=C): return bank(i)[:, H:H + n]
+
+    def ts(out, in0, s1, s2, o0, o1, rd, wr, bk=()):
+        if s2 is None: op("V", lambda: V.tensor_scalar(out, in0, s1, None, o0), rd, wr, bk)
+        else: op("V", lambda: V.tensor_scalar(out, in0, s1, s2, o0, o1), rd, wr, bk)
+
+    def tt(out, a, b, o, rd, wr, bk=()):
+        op("V", lambda: V.tensor_tensor(out, a, b, o), rd, wr, bk)
+
+    def cp(out, a, rd, wr, bk=()):
+        op("V", lambda: V.tensor_copy(out, a), rd, wr, bk)
+
+    def act(out, a, f, rd, wr, bk=(), bias=0.0, scale=1.0):
+        op("S", lambda: S.activation(out, a, f, bias=bias, scale=scale), rd, wr, bk)
+
+    def mm(b, out, m, rhs, start, stop, rd):
+        op("P", lambda: PE.matmul(out, m, rhs, start, stop), rd, [], [b])
+
+    def conv(b, out, wt, src, a, n, start, stop, rd, part=range(16)):
+        for i in part:
+            mm(b, out, T[wt][:, 15 - i:143 - i], T[src][:, a + i:a + n:16], start and i == 0, stop and i == 15, rd + [wt])
+
+    def uni(b, sel, buf, k, h, stop):
+        mm(b, bh(b), T[sel][0:8, :], T[buf][0:8, k * R + h * H:k * R + (h + 1) * H], True, stop, [sel, buf + ("1" if k else "0")])
+
+    def load(e, name, out, src, key, after=()):
+        q = g.sync if e == "Y" else g.scalar
+        op(e, lambda: q.dma_start(out, src), after, [key], done=("ld_" + name, 16))
+        final.append(("ld_" + name, 16))
+    load("Y", "n0", T.n0i[:], T.n0[:], "n0i")
+    load("S", "qd", T.Q[:, 0:W], T.qd[:], "Q")
+    load("Y", "ud", T.UD[0:8, 0:R], T.ud[:, 0:R], "UD0")
+    load("Y", "ua", T.UA[0:8, 0:R], T.ua[:, 0:R], "UA0")
+    load("S", "pt", T.P[:], T.pt[:], "P")
+    load("Y", "spot", T.spi[:], T.spot[:], "spi")
+    load("Y", "ue", T.UD[0:8, R:], T.ud[:, R:], "UD1", ["P"])
+    load("Y", "ub", T.UA[0:8, R:], T.ua[:, R:], "UA1")
+    load("Y", "nx", T.E[:], T.nx[:], "E")
+    load("Y", "vf", T.F[:], T.vf[:], "F")
+
+    def iota(out, pat, cm, key):
+        op("G", lambda: g.iota(out, pat, 0, cm, allow_small_or_imprecise_dtypes=True), [], [key])
+    op("G", lambda: g.iota(T.pi[:, 0:1], [[0, 1]], 0, 1), [], ["pi0"])
+    iota(T.gm[:], [[16, 8], [0, 16]], 0, "gm")
+    iota(T.um[:], [[1, 128]], -1, "um")
+    iota(T.ji[:], [[1, 144]], 0, "ji")
+    def col(k): return T.col[:, k:k + 1]
+    PC, XC, G16, G15, R15, OM, OU, P16, X8 = range(9)
+    eq, mul, add, sub = ALU.is_equal, ALU.mult, ALU.add, ALU.subtract
+    Sign, Relu, Ident, Tanh = ACT.Sign, ACT.Relu, ACT.Identity, ACT.Tanh
+    def scaled(items):
+        for name, src, scale in items:
+            act(T[name][:], T[src][:], Ident, [src], [name], scale=scale)
+    ts(T.pi[:, 1:2], T.pi[:, 0:1], 15, None, ALU.bitwise_and, None, ["pi0"], ["pi1"])
+    cp(col(PC), T.pi[:, 0:1], ["pi0"], ["pc"])
+    cp(col(XC), T.pi[:, 1:2], ["pi1"], ["xc"])
+    ts(col(P16), col(PC), 16.0, None, mul, None, ["pc"], ["p16"])
+    tt(col(G16), col(PC), col(XC), sub, ["pc", "xc"], ["g16"])
+    ts(col(R15), col(XC), 15.0, None, eq, None, ["xc"], ["r15"])
+    ts(col(X8), col(XC), -1.0, -8.0, mul, add, ["xc"], ["x8"])
+    for name, scale in (("sN", -1.0), ("sC", 1.0 / 128), ("sE", 1.0)):
+        ts(T[name][0:8, :], T.gm[0:8, :], T.col[0:8, P16:P16 + 1], scale, eq, mul, ["gm", "p16"], [name])
+    ts(T.blk[:], T.gm[:], col(G16), None, eq, None, ["gm", "g16"], ["blk"])
+    ts(col(G15), col(G16), 15.0, None, add, None, ["g16"], ["g15"])
+    ts(col(OM), col(R15), 8.0, -0.5, mul, add, ["r15"], ["om"])
+    ts(col(OU), col(R15), -8.0, -0.5, mul, add, ["r15"], ["ou"])
+    ts(T.t0[:], T.um[:], 0.0, -0.5, ALU.is_ge, add, ["um"], ["t0"])
+    ts(T.mI[:], T.um[:], 0.0, None, eq, None, ["um"], ["mI"])
+    ts(T.t1[:], T.um[:], 1.0, -1.0, eq, mul, ["um"], ["t1"])
+    ts(T.t2[:], T.um[:], -15.0, -2.0, eq, add, ["um"], ["t2"])
+    tt(T.t0[:], T.t0[:], T.blk[:], mul, ["t0", "blk"], ["t0"])
+    tt(T.t1[:], T.t1[:], T.mI[:], add, ["t1", "mI"], ["t1"])
+    ts(T.t2[:], T.t2[:], col(R15), None, mul, None, ["t2", "r15"], ["t2"])
+    ts(T.mL[:], T.t0[:], 0.0, None, ALU.is_gt, None, ["t0"], ["mL"])
+    ts(T.mS[:], T.um[:], 16.0, None, eq, None, ["um"], ["mS"])
+    tt(T.t1[:], T.t1[:], T.t2[:], add, ["t1", "t2"], ["t1"])
+    scaled((("mP", "mI", 256.0), ("mM", "mI", -256.0), ("fI", "mI", 1.0), ("mH", "mI", W / 2.0), ("mG", "mI", -16.0),
+            ("mB", "blk", 1.0 / 256), ("fB", "blk", -1.0), ("fL", "mL", 128.0), ("mF", "t0", 2.0 ** 25)))
+    for name, sc in (("wW", float(W)), ("wX", 16.0), ("wV", col(OM)), ("wU", col(OU))):
+        ts(T[name][:], T.ji[:], col(G15), sc, eq, mul, ["ji", "g15", "om", "ou"], [name])
+    tt(T.t3[:], T.t1[:], T.blk[:], mul, ["t1", "blk"], ["t3"])
+    scaled((("mO1", "t3", 256.0), ("mO2", "t3", 65536.0)))
+    act(T.t4[:], T.ji[:, 0:32], ACT.Abs, ["ji", "x8"], ["t4"], bias=col(X8))
+    cp(lst(T.NL, 0), T.n0i[:], ["n0i"], ["NL0A", "NL0B"])
+    cp(T.n0f[:], T.n0i[:], ["n0i"], ["n0f"])
+    cp(T.RS[:, 0:C], T.n0f[:], ["n0f"], ["hi0A", "hi0B"])
+    tt(T.RS[:, C:2 * C], T.n0f[:], T.RS[:, 0:C], sub, ["n0f", "hi0A"], ["lo0A", "lo0B"])
+
+    def late():
+        tt(T.mS[:], T.mS[:], T.mI[:], add, ["mS", "mI"], ["mS"])
+        ts(T.OH[:], T.t4[:], 8.0, None, eq, None, ["t4"], ["OH"])
+        ts(T.ON[:], T.t4[:], 8.0, -128.0, ALU.not_equal, mul, ["t4"], ["ON"])
+
+    def send(dst, out, src, sem, rd):
+        es = topo.engines(core, dst)
+        rid, pid = topo.addr(dst, core)
+        sent[0] += len(es)
+        def call():
+            g.remote_dma(out, src, T.sem[sem], T.sem.sent, pid, rid, topo.mask(core, dst))
+        op("G", call, rd, [], done=("sent", 0))
+
+    def send_n(t):
+        if t in (2, 3):
+            dst, frm = (prv, nxt) if t == 2 else (opp, opp)
+            send(dst, lst(T.HI, t - 2), lst(T.NL, t), "ah%d" % (t - 2), ["NL%dA" % t, "NL%dB" % t])
+            arrives("ah%d" % (t - 2), len(topo.engines(frm, core)), ["HI%d" % (t - 2)])
+
+    ne = len(topo.engines(prv, core))
+    win = T.Q[:, 0:W]
+    X, Y, Z, U = (0, 1), (2, 3), (4, 5), (6, 7)
+
+    def steps(t):
+        ni, mi = "NI%d" % t, "mi%d" % t
+        last = t == TK - 1
+        st = {}
+        def ms(buf, a, b): return buf[:, t * 2 * C + a:t * 2 * C + b]
+
+        def half(h):
+            k = "AB"[h]
+            nl = "NL%d" % t + k
+            sl, x, y, z, u = hs(h), X[h], Y[h], Z[h], U[h]
+            r0 = t * RW + 2 * C + h * H
+            qs, rs, ri = T.q1[:, sl], T.RS[:, r0:r0 + H], T.RI[:, r0:r0 + H]
+            kq, kr, ki = "q1" + k, "rs%d" % t + k, "ri%d" % t + k
+            hi, lo = [T.RS[:, (t + 1) * RW + a + 18 * h:(t + 1) * RW + a + 18 * h + 18] for a in (0, C)]
+            own, inc = lst(T.NL, t, 18 * h, 18 * h + 18), lst(T.NI, t, 18 * h, 18 * h + 18)
+            ls = slice(18 * h, 18 * h + 18)
+            of1, nb = T.OF1[:, ls], bank(y)[:, H + 64:H + 82]
+            def tx():
+                a = t * RW if h == 0 else r0
+                rd = [kr] + (["hi%dA" % t, "hi%dB" % t, "lo%dA" % t, "lo%dB" % t] if h == 0 else [])
+                send(nxt, T.RI[:, a:r0 + H], T.RS[:, a:r0 + H], "a%s%d" % ("ab"[h], t), rd)
+                arrives("a%s%d" % ("ab"[h], t), ne, [ki])
+            def dl():
+                mm(u, bh(u), T.mP[:], T.p1[:, sl], True, False, ["mP", "p1" + k])
+                mm(u, bh(u), T.mM[:], qs, False, True, ["mM", kq])
+            def qq():
+                if h == 0 and k not in FB: cp(T.q2[:, sl], win.indirect(inc), ["Q", ni], ["q2" + k])
+                else: act(T.q2[:, sl], win.indirect(inc), Ident, ["Q", ni], ["q2" + k])
+            def sq():
+                if k in FB: tt(T.sq[:, sl], win.indirect(inc), T.sb[:, sl], mul, ["Q", ni, "sb" + k], ["sq" + k])
+                else: tt(T.sq[:, sl], T.q2[:, sl], bh(y), mul, ["q2" + k], ["sq" + k], [y])
+            def sgm():
+                mm(z, bl(z, 18), T.mS[:], T.VL[:, ls], True, True, ["mS", "vl" + k])
+                mm(y, nb, T.mI[:], T.VL[:, ls], True, False, ["mI", "vl" + k])
+            def oe():
+                mm(u, bh(u), T.mI[:], T.ec[:, sl], True, False, ["mI", "ec"])
+                mm(u, bh(u), T.mI[:], T.og[:, sl], False, True, ["mI", "og" + k])
+            d = {
+                "a": lambda: uni(x, "sN", "UD", 2 * t, h, False),
+                "c": lambda: uni(y, "sC", "UA", 3 * t, h, True),
+                "p": lambda: mm(u, bl(u, 18), T.fI[:], T.sp1[:, t * C + 18 * h:t * C + 18 * h + 18], True, False, ["fI", "sp1"]),
+                "gq": lambda: cp(qs, win.indirect(own), ["Q", nl], [kq]),
+                "gp": lambda: act(T.p1[:, sl], T.P[:].indirect(own), Ident, ["P", nl], ["p1" + k]),
+                "dl": dl,
+                "rl": lambda: act(rs, bh(u), Relu, [], [kr], [u]),
+                "tx": tx,
+                "Lq": lambda: mm(x, bh(x), T.mL[:], qs, False, True, ["mL", kq]),
+                "Ip": lambda: mm(z, bh(z), T.mI[:], T.p1[:, sl], True, False, ["mI", "p1" + k]),
+                "sg": lambda: act(T.s1[:, sl], bh(x), Sign, [], ["s1" + k], [x], bias=-0.5),
+                "cq": lambda: tt(T.cq[:, sl], qs, bh(y), mul, [kq], ["cq" + k], [y]),
+                "pm": lambda: mm(z, bh(z), T.mO1[:], T.s1[:, sl], False, True, ["mO1", "s1" + k]),
+                "f": lambda: tt(T.fo1[:, sl], T.cq[:, sl], bh(z), ALU.is_lt, ["cq" + k], ["fo1" + k], [z]),
+                "cv": lambda: conv(u, bl(u, 18), "wW", "fo1", h * H, H, False, True, ["fo1" + k]),
+                "of": lambda: cp(of1, bl(u, 18), [], ["of1" + k], [u]),
+                "x1": lambda: cp(T.Q[:, 0:2 * W].indirect(of1), T.p1[:, sl], ["of1" + k, "p1" + k], ["Q"]),
+                "g2": lambda: act(T.p2[:, sl], T.P[:].indirect(inc), Ident, ["P", ni], ["p2" + k]),
+                "b": lambda: uni(z, "sN", "UD", 2 * t + 1, h, False),
+                "d": lambda: uni(u, "sC", "UA", 3 * t + 1, h, True),
+                "e": lambda: uni(y, "sE", "UA", 3 * t + 2, h, True),
+                "S": lambda: mm(y, bh(y), T.mB[:], ri, True, True, ["mB", ki]),
+                "Ir": lambda: mm(x, bh(x), T.mI[:], ri, True, True, ["mI", ki]),
+                "qq": qq, "sq": sq,
+                "L2": lambda: mm(z, bh(z), T.mL[:], T.q2[:, sl], False, True, ["mL", "q2" + k]),
+                "s2": lambda: act(T.s2[:, sl], bh(z), Sign, [], ["s2" + k], [z], bias=-0.5),
+                "wr": lambda: tt(T.wr[:, sl], bh(x), T.sq[:, sl], sub, ["sq" + k], ["wr" + k], [x]),
+                "rw": lambda: act(T.wp[:, sl], T.wr[:, sl], Relu, ["wr" + k], ["wp" + k]),
+                "I2": lambda: mm(x, bh(x), T.mI[:], ri, True, False, ["mI", ki]),
+                "p2": lambda: mm(x, bh(x), T.mO2[:], T.s2[:, sl], False, True, ["mO2", "s2" + k]),
+                "Lw": lambda: mm(z, bh(z), T.fL[:], T.wp[:, sl], True, False, ["fL", "wp" + k]),
+                "dq": lambda: tt(T.dq[:, sl], T.sq[:, sl], bh(u), mul, ["sq" + k], ["dq" + k], [u]),
+                "f2": lambda: tt(T.fo2[:, sl], T.dq[:, sl], bh(x), ALU.is_lt, ["dq" + k], ["fo2" + k], [x]),
+                "ew": lambda: tt(T.ew[:, sl], T.wp[:, sl], bh(y), mul, ["wp" + k], ["ew" + k], [y]),
+                "Ow": lambda: mm(z, bh(z), T.fB[:], T.ew[:, sl], False, False, ["fB", "ew" + k]),
+                "ov": lambda: mm(z, bh(z), T.mF[:], T.fo2[:, sl], False, True, ["mF", "fo2" + k]),
+                "sv": lambda: act(T.sv[:, sl], bh(z), Sign, [], ["sv" + k], [z], bias=-0.5),
+                "vp": lambda: mm(y, bl(y, 18), T.mG[:], ms(T.MI, C + 18 * h, C + 18 * h + 18), True, False, ["mG", mi]),
+                "cvv": lambda: conv(y, bl(y, 18), "wU", "sv", h * H, H, False, True, ["sv" + k]),
+                "vmx": lambda: tt(T.VL[:, ls], bl(y, 18), ms(T.MI, 18 * h, 18 * h + 18), ALU.max, [mi], ["vl" + k], [y]),
+                "sgm": sgm,
+                "sgc": lambda: cp(T.SG[:, ls], bl(z, 18), [], ["sg" + k], [z]),
+                "cve": lambda: conv(y, nb, "wX", "eo", h * H, H, False, True, ["eo" + k]),
+                "nl": lambda: cp(lst(T.NL, t + 1, 18 * h, 18 * h + 18), nb, [], ["NL%d" % (t + 1) + k], [y]),
+                "yn": lambda: act(T.YN[:, t * C + 18 * h:t * C + 18 * h + 18], nb, Ident, [], ["yn%d" % t + k], [y]),
+                "hi": lambda: act(hi, nb, Ident, [], ["hi%d" % (t + 1) + k], [y]),
+                "lo": lambda: tt(lo, nb, hi, sub, ["hi%d" % (t + 1) + k], ["lo%d" % (t + 1) + k], [y]),
+            }
+            if k in FB: d["Sc"] = lambda: act(T.sb[:, sl], bh(y), Ident, [], ["sb" + k], [y])
+            if k in FD and not last:
+                d["og"] = lambda: act(T.og[:, sl], T.ON[:].indirect(T.SG[:, ls]), Ident, ["ON", "sg" + k], ["og" + k])
+                d["oe"] = oe
+                d["or"] = lambda: act(T.eo[:, sl], bh(u), Relu, [], ["eo" + k], [u])
+            else:
+                d["eo"] = lambda: tt(T.eo[:, sl], T.OH[:].indirect(T.SG[:, ls]), T.ec[:, sl], mul, ["OH", "sg" + k, "ec"], ["eo" + k])
+            if last:
+                d["k"] = lambda: tt(T.hx[:, sl], T.F[:].indirect(inc), T.hh[:, sl], add, ["F", ni, "hh" + k], ["hx" + k])
+                d["tk"] = lambda: act(T.hh[:, sl], T.hx[:, sl], Tanh, ["hx" + k], ["hh" + k])
+            for name in d:
+                st[name + k] = d[name]
+        half(0)
+        half(1)
+
+        def msg():
+            act(ms(T.MS, 0, C), bl(Y[0]), Ident, [], ["msa%d" % t], [Y[0]], bias=-16.0)
+            act(ms(T.MS, C, 2 * C), bl(Y[0]), Sign, [], ["msb%d" % t], [Y[0]], bias=-15.5)
+            send(nxt, ms(T.MI, 0, 2 * C), ms(T.MS, 0, 2 * C), "am%d" % t, ["msa%d" % t, "msb%d" % t])
+            arrives("am%d" % t, ne, [mi])
+        def nm():
+            mm(X[0], bl(X[0]), T.mI[:], T.RI[:, t * RW:t * RW + C], True, False, ["mI", "ri%dA" % t])
+            mm(X[0], bl(X[0]), T.mI[:], T.RI[:, t * RW + C:t * RW + 2 * C], False, True, ["mI", "ri%dA" % t])
+        def o2c():
+            conv(U[0], bl(U[0]), "wW", "fo2", 0, R, False, False, ["fo2A", "fo2B"])
+            mm(U[0], bl(U[0]), T.mH[:], ms(T.MI, C, 2 * C), False, True, ["mH", mi])
+        def x2(j):
+            a, b = X2CUT[j], X2CUT[j + 1]
+            if b > a: cp(T.Q[:].indirect(T.OF2[:, a:b]), T.p2[:, 16 * a:16 * b], ["of2", "p2A", "p2B"], ["Q"])
+        fo1, hh, hx = ["fo1A"], ["hhA", "hhB"], ["hxA", "hxB"]
+        st.update({
+            "sn": lambda: send_n(t),
+            "c1a": lambda: conv(U[0], bl(U[0], 18), "wW", "fo1", 0, H, False, True, fo1, range(0, 6)),
+            "c1b": lambda: conv(U[0], bl(U[0], 18), "wW", "fo1", 0, H, False, True, fo1, range(6, 16)),
+            "cd1": lambda: conv(Y[0], bl(Y[0]), "wV", "s1", 0, R, True, False, ["s1A", "s1B"]),
+            "cd2": lambda: conv(Y[0], bl(Y[0]), "wX", "fo1", 0, R, False, True, ["fo1A", "fo1B"]),
+            "msg": msg, "nm": nm,
+            "nc": lambda: cp(lst(T.NI, t), bl(X[0]), [], [ni], [X[0]]),
+            "ecg": lambda: act(T.ec[:], T.E[:].indirect(lst(T.NI, t)), Ident, ["E", ni], ["ec"]),
+            "o2p": lambda: mm(U[0], bl(U[0]), T.fI[:], T.sp2[:, t * C:(t + 1) * C], True, False, ["fI", "sp2"]),
+            "o2c": o2c,
+            "of2": lambda: cp(T.OF2[:, 0:C], bl(U[0]), [], ["of2"], [U[0]]),
+            "x2a": lambda: x2(0), "x2b": lambda: x2(1), "x2c": lambda: x2(2),
+        })
+        if t == 1:
+            st["th"] = lambda: act(T.hh[:], T.F[:].indirect(lst(T.NL, 1)), Tanh, ["F", "NL1A", "NL1B"], hh)
+        if t in (2, 3):
+            st["hg"] = lambda: act(T.hx[:], T.F[:].indirect(lst(T.HI, t - 2)), Ident, ["F", "HI%d" % (t - 2)], hx)
+            st["hd"] = lambda: op("G", lambda: g.dma_start(T.hh[:], T.hx[:], accum_op=add), hx + hh, hh, done=("hd%d" % t, 16))
+        if t in (3, 4):
+            st["th"] = lambda: act(T.hh[:], T.hh[:], Tanh, hh, hh)
+        if last:
+            for name in ("o2p", "o2c", "of2", "x2a", "x2b", "x2c", "hiA", "hiB", "loA", "loB", "g2A", "g2B"):
+                del st[name]
+        return st
+
+    def out_h(k, a, b):
+        sl = slice(16 * a, 16 * b)
+        tt(T.hx[:, sl], T.F[:].indirect(lst(T.NL, TK, a, b)), T.hh[:, sl], add, ["F", "NL%d" % TK + k, "hh" + k], ["hz%d" % a])
+        act(T.wr[:, sl], T.hx[:, sl], Tanh, ["hz%d" % a], ["ho%d" % a, "wr" + k])
+        op("Y", lambda: g.sync.dma_start(T.yh[:, sl], T.wr[:, sl]), ["ho%d" % a], [], done=("stored", 16))
+
+    def out_b():
+        op("Y", lambda: g.sync.dma_start(T.yn[:], T.YN[:]), ["yn%d%s" % (t, k) for t in range(TK) for k in "AB"], [],
+           done=("stored", 16))
+        for a, b in zip(TAIL, TAIL[1:]): out_h("B", a, b)
+
+    every = [steps(t) for t in range(TK)] + [{"gqA": lambda: out_h("A", 0, 18), "gqB": out_b}]
+    every[0]["spc"] = lambda: cp(T.sp1[:], T.spi[:], ["spi"], ["sp1"])
+    every[0]["spd"] = lambda: ts(T.sp2[:], T.sp1[:], W / 2.0, None, add, None, ["sp1"], ["sp2"])
+    every[0]["late"] = late
+    for name in FIRST:
+        every[0][name]()
+    for t in range(TK):
+        for name in ORDER:
+            st = every[t + 1] if name[0] == "+" else every[t]
+            if name.lstrip("+") in st: st[name.lstrip("+")]()
+    final.append(("stored", 16 * (len(TAIL) + 1)))
+    final.append(("sent", sent[0]))
+    emit(g, T, ops, final)

@@ -1,58 +1,65 @@
+from concourse.bass import DstId, RemoteDMATransfer
 from concourse.mybir import AluOpType as ALU, ActivationFunctionType as ACT
 
 W, R, TK, C = 1280, 576, 5, 36
 H = R // 2
-RW = 2 * C + R
 LS = 40
+UNIT = 4096.0
 
 SCRATCH = {
-    "Q": ("sbuf", [128, 3 * W], "bfloat16"), "P": ("sbuf", [128, W], "bfloat16"),
+    "Q": ("sbuf", [128, 2 * W], "float32"), "Q0": ("sbuf", [128, W], "bfloat16"), "P": ("sbuf", [128, W], "bfloat16"),
     "E": ("sbuf", [128, W], "bfloat16"), "F": ("sbuf", [128, W], "bfloat16"),
-    "UD": ("sbuf", [128, 2 * TK * R], "bfloat16"), "UA": ("sbuf", [128, 3 * TK * R], "bfloat16"),
-    "n0i": ("sbuf", [128, C], "int32"), "n0f": ("sbuf", [128, C], "float32"), "spi": ("sbuf", [128, TK * C], "int32"),
-    "sp1": ("sbuf", [128, TK * C], "float32"), "sp2": ("sbuf", [128, TK * C], "float32"),
-    "RS": ("sbuf", [128, (TK + 1) * RW], "bfloat16"), "RI": ("sbuf", [128, TK * RW], "bfloat16"),
-    "NL": ("sbuf", [128, (TK + 1) * LS], "uint16"), "NI": ("sbuf", [128, TK * LS], "uint16"),
+    "UD": ("sbuf", [128, 2 * TK * R], "bfloat16"), "UC": ("sbuf", [128, 3 * TK * R], "bfloat16"),
+    "UB": ("sbuf", [128, 2 * TK * R], "bfloat16"),
+    "n0i": ("sbuf", [128, C], "int32"), "spi": ("sbuf", [128, TK * C], "int32"),
+    "sp1": ("sbuf", [128, TK * C], "float32"), "sph": ("sbuf", [128, TK * C], "float16"),
+    "NL": ("sbuf", [128, (TK + 1) * C], "uint16"), "NI": ("sbuf", [128, TK * LS], "uint16"),
     "HI": ("sbuf", [128, 2 * LS], "uint16"),
-    "MS": ("sbuf", [128, TK * 2 * C], "bfloat16"), "MI": ("sbuf", [128, TK * 2 * C], "bfloat16"),
-    "VL": ("sbuf", [128, LS], "bfloat16"), "OF1": ("sbuf", [128, LS], "uint16"), "OF2": ("sbuf", [128, LS], "uint16"),
-    "SG": ("sbuf", [128, LS], "uint16"), "YN": ("sbuf", [128, TK * C], "float32"),
+    "KB": ("sbuf", [128, C], "bfloat16"), "OF1": ("sbuf", [128, C], "uint16"), "OF2": ("sbuf", [128, C], "uint16"),
+    "SG": ("sbuf", [128, C], "uint16"), "YN": ("sbuf", [128, TK * C], "float32"),
     "ji": ("sbuf", [128, 144], "bfloat16"), "pi": ("sbuf", [128, 4], "int32"), "col": ("sbuf", [128, 16], "bfloat16"),
-    "OH": ("sbuf", [128, 32], "bfloat16"), "ON": ("sbuf", [128, 32], "bfloat16"), "t4": ("sbuf", [128, 32], "bfloat16"),
+    "OH": ("sbuf", [128, 32], "bfloat16"), "t4": ("sbuf", [128, 32], "bfloat16"), "hI": ("sbuf", [128, 128], "float16"),
 }
-for _n in ("p1", "q1", "s1", "fo1", "p2", "q2", "s2", "fo2", "sv", "ec", "eo", "og", "sb"):
+for _n in ("p1", "q1", "fo1", "DI", "FI"):
+    SCRATCH[_n] = ("sbuf", [128, TK * R], "bfloat16")
+for _n in ("s1", "rr", "q2", "s2", "fo2", "sv", "ec", "eo"):
     SCRATCH[_n] = ("sbuf", [128, R], "bfloat16")
-for _n in ("cq", "sq", "wr", "wp", "ew", "dq", "hh", "hx"):
+for _n in ("cq", "p2", "mn", "th", "dq", "hh", "hx", "ho"):
     SCRATCH[_n] = ("sbuf", [128, R], "float32")
-for _n in ("mL", "mI", "mO1", "mO2", "mP", "mM", "mB", "mF", "mH", "mG", "mS", "sN", "sC", "sE",
-           "um", "gm", "blk", "t0", "t1", "t2", "t3"):
+for _n in ("mL", "mN", "mI", "mP", "mR", "mW", "mO1", "mO2", "mB", "mF", "mA", "mT", "sN", "sC",
+           "um", "gm", "blk", "t0", "t1", "t2", "t3", "t5"):
     SCRATCH[_n] = ("sbuf", [128, 128], "bfloat16")
-for _n in ("fL", "fB", "fI"):
+for _n in ("fL", "fB"):
     SCRATCH[_n] = ("sbuf", [128, 128], "float32")
-for _n in ("wV", "wW", "wX", "wU"):
+for _n in ("wK", "wW", "wX", "w0"):
     SCRATCH[_n] = ("sbuf", [128, 144], "bfloat16")
+SCRATCH["ti"] = ("sbuf", [128, 128], "int32")
 for _i in range(8):
     SCRATCH["b%d" % _i] = ("psum", [128, 512], "float32")
 
 LOADS = ["n0", "qd", "pt", "ud", "ue", "ua", "ub", "spot", "nx", "vf"]
-SEMAPHORES = (["cV", "cS", "cP", "cG", "sent", "stored", "ah0", "ah1", "hd2", "hd3"] + ["ld_" + n for n in LOADS]
-              + ["%s%d" % (k, t) for t in range(TK) for k in ("aa", "ab", "am")])
+SEMAPHORES = (["cV", "cS", "cP", "cG", "sent", "stored", "ah2", "ah3", "hd2", "hd3"] + ["ld_" + n for n in LOADS]
+              + ["%s%d" % (k, t) for t in range(TK) for k in ("an", "dA", "dB", "fA", "fB", "ub")])
 
-X2CUT = [0, 36, 36, 36]
+ONV = ["gqA", "qqB", "rrA", "rrB"]
+WHOLE = ""
+X2CUT = [0, 12, 24, 36]
 TAIL = [18, 28, 36]
-FB = "A"
-FD = ""
-FIRST = """aA cA aB cB gqA gqB LqA LqB sgA cqA gpA dlA rlA IpA pmA txA gpB dlB IpB spc pA spd late""".split()
-ORDER = """fA sgB c1a rlB pmB cqB th fB c1b pB ofA cd1 txB cvB x1A cd2 bB msg ofB dA SA x1B ScA nm bA nc dB qqA sn o2p eA IrA L2A SB
-sqA wrA IrB qqB sqB I2A dqA L2B wrB s2A rwA p2A s2B rwB eB LwA dqB f2A g2B I2B p2B f2B ewA g2A LwB o2c ewB OwA kB ecg ovA OwB ovB svA
-vpA cvvA kA tkB of2 svB hg x2a vmxA +aA vpB sgmA cvvB sgcA +aB eoA vmxB sgmB sgcB cveA eoB nlA hiA hd tkA +gqA cveB nlB ynA +gpA +LqA
-hiB +sgA +dlA +IpA +rlA loA loB ynB +txA +cA +gpB +pmA +cB +gqB +pA +LqB +dlB +IpB +cqA""".split()
+FIRST = """bc aA aB cA cB gpA gqA sn IpA gqB cqA LqA LqB sgA gpB spc qf pA pB pmA IpB fA cqB txA txB sgB pmB late fB tfA tfB cvA bA ofA x1A""".split()
+ORDER = """cvB ofB th x1B rrA rrB SA SB BrA BrB I2A AA hg ecg g2 qqA qqB bB L2A sqA s2A mnA dqA hd L2B sqB s2B p2A LrA BmA f2A mnB I2B AB p2B dqB
+LmA f2B ovA o2p o2c tA svA of2 LrB BmB LmB ovB cvkA x2a kA tB svB sgcA kbA eoA altA cvkB x2b kB tkA cveA sgcB kbB eoB altB nlA x2c tkB cveB nlB
+yn +bc +sn +aA +aB +cA +cB +gpA +gqA +gqB +txA +pA +LqA +sgA +IpA +LqB +gpB +pmA +cqA +cqB +txB +sgB +fA +tfA +IpB +pmB +cvA +fB +tfB +ofA
++x1A +bA +pB""".split()
+ONV = ["gpA", "gqB", "qqB"]
+FIRST = """aA qf gpB gqA gqB cB aB cA IpB sn LqB LqA spc gpA txA cqA IpA cqB kA sgA txB pmA pB fA pA sgB pmB fB late th bA rrA cvA cvB bB ofB rrB SA BrB ofA x1A BrA I2A x1B qqA L2A qqB sqA s2A SB L2B""".split()
+ORDER = """kB I2B o2p mnA LrA bc s2B BmA tfA ecg sqB hg LrB mnB BmB dqB AA dqA tfB tB p2A AB p2B f2A f2B tA LmA ovA svA g2 o2c cvkA of2 x2a LmB sgcA kbA x2b ovB svB cvkB eoA sgcB eoB x2c hd altA kbB cveA altB cveB nlA +gqA +cB +aA +gpA nlB +gpB +cA +LqA +txA tkA +gqB +sgA +IpA +cqA +aB +LqB +cqB +sgB +pmA +fA +IpB +sn +pmB +rrA +fB +txB tkB +pA +pB +yn +cvA ynB +ofA +x1A +cvB +I2A +SA +ofB +x1B +th +bA +kA +qqA +bB +BrA +qqB +rrB +L2A +L2B +s2A +SB +BrB +sqA ynA""".split()
+LAST = """I2B bc tfA ecg s2B LrA mnA sqB dqA BmA tA mnB LmA LrB dqB AA p2A BmB f2A tfB kB AB p2B f2B ovA LmB svA ovB tB svB cvkA sgcA cvkB eoA kbA tkB kbB sgcB altA eoB cveA altB tkA nlA cveB +gqA nlB ynB ynA +sn +gqB""".split()
 
 
 def emit(g, T, ops, final):
     queue = {"V": g.vector, "S": g.scalar, "P": g.tensor, "G": g, "Y": g.sync}
     last_w, readers, last_b, deps = {}, {}, {}, []
-    for i, (e, fn, rd, wr, bk, done) in enumerate(ops):
+    for i, (e, fn, rd, wr, bk, done, name) in enumerate(ops):
         d = set()
         for k in rd:
             d.add(last_w[k])
@@ -61,19 +68,19 @@ def emit(g, T, ops, final):
         for k in bk:
             if k in last_b and ops[last_b[k]][0] != e: d.add(last_b[k])
         d.discard(i)
-        deps.append(d)
+        deps.append({j for j in d if not (e == "P" and ops[j][0] == "P")})
         for k in rd: readers.setdefault(k, []).append(i)
         for k in wr:
             last_w[k] = i
             readers[k] = []
         for k in bk: last_b[k] = i
     pos, cnt = [], {}
-    for e, fn, rd, wr, bk, done in ops:
-        cnt[e] = cnt.get(e, 0) + 1
-        pos.append(cnt[e])
+    for op in ops:
+        cnt[op[0]] = cnt.get(op[0], 0) + 1
+        pos.append(cnt[op[0]])
     know = {e: {} for e in list(queue) + ["X"]}
     clock, waits, needed = [], [], set()
-    for i, (e, fn, rd, wr, bk, done) in enumerate(ops):
+    for i, (e, fn, rd, wr, bk, done, name) in enumerate(ops):
         w = []
         for j in sorted(deps[i], reverse=True):
             key = ops[j][5][0] if ops[j][5] is not None else ops[j][0]
@@ -87,7 +94,7 @@ def emit(g, T, ops, final):
         c[done[0] if done is not None else e] = pos[i]
         clock.append(c)
     val, n, seen = {}, {}, {}
-    for i, (e, fn, rd, wr, bk, done) in enumerate(ops):
+    for i, (e, fn, rd, wr, bk, done, name) in enumerate(ops):
         for j in waits[i]:
             s, v = ops[j][5] if ops[j][5] is not None else ("c" + ops[j][0], val[j])
             queue[e].wait_ge(T.sem[s], v)
@@ -110,11 +117,11 @@ def rank_program(g, core, T, topo):
         return
     N = len(T.cores)
     nxt, prv, opp = T.cores[(rank + 1) % N], T.cores[(rank - 1) % N], T.cores[(rank + 2) % N]
-    ops, final, sent = [], [], [0]
+    ops, final, sent, now = [], [], [0], ["setup"]
     V, S, PE = g.vector, g.scalar, g.tensor
 
     def op(e, fn, rd, wr, bk=(), done=None):
-        ops.append((e, fn, list(rd), list(wr), list(bk), done))
+        ops.append((e, fn, list(rd), list(wr), list(bk) + [k[0] for k in list(rd) + list(wr) if isinstance(k, tuple)], done, now[0]))
 
     def arrives(sem, count, keys):
         op("X", None, [], keys, done=(sem, count))
@@ -122,47 +129,62 @@ def rank_program(g, core, T, topo):
 
     def hs(h): return slice(h * H, (h + 1) * H)
     def lst(buf, k, a=0, b=C): return buf[:, k * LS + a:k * LS + b]
+    def nlst(k, a=0, b=C): return T.NL[:, k * C + a:k * C + b]
     def bank(i): return T["b%d" % i]
     def bh(i): return bank(i)[:, 0:H]
-    def bl(i, n=C): return bank(i)[:, H:H + n]
+    def bl(i, n=C, a=0): return bank(i)[:, H + a:H + a + n]
 
-    def ts(out, in0, s1, s2, o0, o1, rd, wr, bk=()):
-        if s2 is None: op("V", lambda: V.tensor_scalar(out, in0, s1, None, o0), rd, wr, bk)
-        else: op("V", lambda: V.tensor_scalar(out, in0, s1, s2, o0, o1), rd, wr, bk)
+    eq, mul, add, sub = ALU.is_equal, ALU.mult, ALU.add, ALU.subtract
+    Sign, Relu, Ident, Tanh = ACT.Sign, ACT.Relu, ACT.Identity, ACT.Tanh
 
-    def tt(out, a, b, o, rd, wr, bk=()):
-        op("V", lambda: V.tensor_tensor(out, a, b, o), rd, wr, bk)
+    def ts(out, in0, s1, s2, o0, o1, rd, wr):
+        if s2 is None: op("V", lambda: V.tensor_scalar(out, in0, s1, None, o0), rd, wr)
+        else: op("V", lambda: V.tensor_scalar(out, in0, s1, s2, o0, o1), rd, wr)
 
-    def cp(out, a, rd, wr, bk=()):
-        op("V", lambda: V.tensor_copy(out, a), rd, wr, bk)
+    def tt(out, a, b, o, rd, wr):
+        op("V", lambda: V.tensor_tensor(out, a, b, o), rd, wr)
 
-    def act(out, a, f, rd, wr, bk=(), bias=0.0, scale=1.0):
-        op("S", lambda: S.activation(out, a, f, bias=bias, scale=scale), rd, wr, bk)
+    def cp(out, a, rd, wr):
+        op("V", lambda: V.tensor_copy(out, a), rd, wr)
 
-    def mm(b, out, m, rhs, start, stop, rd):
-        op("P", lambda: PE.matmul(out, m, rhs, start, stop), rd, [], [b])
+    def act(out, a, f, rd, wr, bias=0.0, scale=1.0):
+        op("S", lambda: S.activation(out, a, f, bias=bias, scale=scale), rd, wr)
 
-    def conv(b, out, wt, src, a, n, start, stop, rd, part=range(16)):
-        for i in part:
-            mm(b, out, T[wt][:, 15 - i:143 - i], T[src][:, a + i:a + n:16], start and i == 0, stop and i == 15, rd + [wt])
+    def scale_to(name, out, a, scale, rd, wr):
+        if name in ONV: ts(out, a, scale, None, mul, None, rd, wr)
+        else: act(out, a, Ident, rd, wr, scale=scale)
+
+    def mm(key, out, m, rhs, start, stop, rd):
+        op("P", lambda: PE.matmul(out, m, rhs, start, stop), rd + ([] if start else [key]), [key, (key[0], "group")])
+
+    def conv(key, out, wt, src, a, n, start, stop, rd):
+        for i in range(16):
+            mm(key, out, T[wt][:, 15 - i:143 - i], T[src][:, a + i:a + n:16], start and i == 0, stop and i == 15, rd + [wt])
 
     def uni(b, sel, buf, k, h, stop):
-        mm(b, bh(b), T[sel][0:8, :], T[buf][0:8, k * R + h * H:k * R + (h + 1) * H], True, stop, [sel, buf + ("1" if k else "0")])
+        mm((b, "h"), bh(b), T[sel][0:8, :], T[buf][0:8, k * R + h * H:k * R + (h + 1) * H], True, stop, [sel, buf + ("1" if k else "0")])
 
     def load(e, name, out, src, key, after=()):
         q = g.sync if e == "Y" else g.scalar
         op(e, lambda: q.dma_start(out, src), after, [key], done=("ld_" + name, 16))
         final.append(("ld_" + name, 16))
     load("Y", "n0", T.n0i[:], T.n0[:], "n0i")
-    load("S", "qd", T.Q[:, 0:W], T.qd[:], "Q")
+    load("S", "qd", T.Q0[:], T.qd[:], "Q0")
+    load("Y", "pt", T.P[:], T.pt[:], "P")
     load("Y", "ud", T.UD[0:8, 0:R], T.ud[:, 0:R], "UD0")
-    load("Y", "ua", T.UA[0:8, 0:R], T.ua[:, 0:R], "UA0")
-    load("S", "pt", T.P[:], T.pt[:], "P")
+    load("Y", "ua", T.UC[0:8, 0:R], T.ua[:, 0:R], "UC0")
     load("Y", "spot", T.spi[:], T.spot[:], "spi")
     load("Y", "ue", T.UD[0:8, R:], T.ud[:, R:], "UD1", ["P"])
-    load("Y", "ub", T.UA[0:8, R:], T.ua[:, R:], "UA1")
     load("Y", "nx", T.E[:], T.nx[:], "E")
-    load("Y", "vf", T.F[:], T.vf[:], "F")
+
+    def spread(t):
+        for x in range(16):
+            op("Y", lambda x=x: g.sync.dma_start(T.UB[x:128:16, 2 * t * R:2 * (t + 1) * R], T.ua[:, (3 * t + 1) * R:3 * (t + 1) * R]),
+               ["NL%dA" % t], ["ub%d" % t] if x == 15 else [], done=("ub%d" % t, 256))
+        final.append(("ub%d" % t, 256))
+        if t == 0:
+            load("Y", "ub", T.UC[0:8, 3 * R:], T.ua[:, 3 * R:], "UC1")
+            load("Y", "vf", T.F[:], T.vf[:], "F")
 
     def iota(out, pat, cm, key):
         op("G", lambda: g.iota(out, pat, 0, cm, allow_small_or_imprecise_dtypes=True), [], [key])
@@ -171,9 +193,7 @@ def rank_program(g, core, T, topo):
     iota(T.um[:], [[1, 128]], -1, "um")
     iota(T.ji[:], [[1, 144]], 0, "ji")
     def col(k): return T.col[:, k:k + 1]
-    PC, XC, G16, G15, R15, OM, OU, P16, X8 = range(9)
-    eq, mul, add, sub = ALU.is_equal, ALU.mult, ALU.add, ALU.subtract
-    Sign, Relu, Ident, Tanh = ACT.Sign, ACT.Relu, ACT.Identity, ACT.Tanh
+    PC, XC, G16, G15, R15, OM, G31, P16, X8 = range(9)
     def scaled(items):
         for name, src, scale in items:
             act(T[name][:], T[src][:], Ident, [src], [name], scale=scale)
@@ -183,152 +203,151 @@ def rank_program(g, core, T, topo):
     ts(col(P16), col(PC), 16.0, None, mul, None, ["pc"], ["p16"])
     tt(col(G16), col(PC), col(XC), sub, ["pc", "xc"], ["g16"])
     ts(col(R15), col(XC), 15.0, None, eq, None, ["xc"], ["r15"])
-    ts(col(X8), col(XC), -1.0, -8.0, mul, add, ["xc"], ["x8"])
-    for name, scale in (("sN", -1.0), ("sC", 1.0 / 128), ("sE", 1.0)):
-        ts(T[name][0:8, :], T.gm[0:8, :], T.col[0:8, P16:P16 + 1], scale, eq, mul, ["gm", "p16"], [name])
+    ts(T.sN[0:8, :], T.gm[0:8, :], T.col[0:8, P16:P16 + 1], -1.0, eq, mul, ["gm", "p16"], ["sN"])
     ts(T.blk[:], T.gm[:], col(G16), None, eq, None, ["gm", "g16"], ["blk"])
     ts(col(G15), col(G16), 15.0, None, add, None, ["g16"], ["g15"])
-    ts(col(OM), col(R15), 8.0, -0.5, mul, add, ["r15"], ["om"])
-    ts(col(OU), col(R15), -8.0, -0.5, mul, add, ["r15"], ["ou"])
     ts(T.t0[:], T.um[:], 0.0, -0.5, ALU.is_ge, add, ["um"], ["t0"])
     ts(T.mI[:], T.um[:], 0.0, None, eq, None, ["um"], ["mI"])
     ts(T.t1[:], T.um[:], 1.0, -1.0, eq, mul, ["um"], ["t1"])
     ts(T.t2[:], T.um[:], -15.0, -2.0, eq, add, ["um"], ["t2"])
+    act(T.sC[0:8, :], T.sN[0:8, :], Ident, ["sN"], ["sC"], scale=UNIT / 128)
+    scaled((("mP", "mI", UNIT),))
     tt(T.t0[:], T.t0[:], T.blk[:], mul, ["t0", "blk"], ["t0"])
     tt(T.t1[:], T.t1[:], T.mI[:], add, ["t1", "mI"], ["t1"])
     ts(T.t2[:], T.t2[:], col(R15), None, mul, None, ["t2", "r15"], ["t2"])
-    ts(T.mL[:], T.t0[:], 0.0, None, ALU.is_gt, None, ["t0"], ["mL"])
-    ts(T.mS[:], T.um[:], 16.0, None, eq, None, ["um"], ["mS"])
+    ts(T.mN[:], T.t0[:], 0.0, -UNIT, ALU.is_gt, mul, ["t0"], ["mN"])
     tt(T.t1[:], T.t1[:], T.t2[:], add, ["t1", "t2"], ["t1"])
-    scaled((("mP", "mI", 256.0), ("mM", "mI", -256.0), ("fI", "mI", 1.0), ("mH", "mI", W / 2.0), ("mG", "mI", -16.0),
-            ("mB", "blk", 1.0 / 256), ("fB", "blk", -1.0), ("fL", "mL", 128.0), ("mF", "t0", 2.0 ** 25)))
-    for name, sc in (("wW", float(W)), ("wX", 16.0), ("wV", col(OM)), ("wU", col(OU))):
-        ts(T[name][:], T.ji[:], col(G15), sc, eq, mul, ["ji", "g15", "om", "ou"], [name])
+    ts(T.wW[:], T.ji[:], col(G15), float(W), eq, mul, ["ji", "g15"], ["wW"])
     tt(T.t3[:], T.t1[:], T.blk[:], mul, ["t1", "blk"], ["t3"])
-    scaled((("mO1", "t3", 256.0), ("mO2", "t3", 65536.0)))
-    act(T.t4[:], T.ji[:, 0:32], ACT.Abs, ["ji", "x8"], ["t4"], bias=col(X8))
-    cp(lst(T.NL, 0), T.n0i[:], ["n0i"], ["NL0A", "NL0B"])
-    cp(T.n0f[:], T.n0i[:], ["n0i"], ["n0f"])
-    cp(T.RS[:, 0:C], T.n0f[:], ["n0f"], ["hi0A", "hi0B"])
-    tt(T.RS[:, C:2 * C], T.n0f[:], T.RS[:, 0:C], sub, ["n0f", "hi0A"], ["lo0A", "lo0B"])
+    scaled((("mO1", "t3", 256.0),))
+    cp(T.hI[:], T.mI[:], ["mI"], ["hI"])
+    cp(nlst(0), T.n0i[:], ["n0i"], ["NL0A", "NL0B"])
 
     def late():
-        tt(T.mS[:], T.mS[:], T.mI[:], add, ["mS", "mI"], ["mS"])
+        scaled((("mB", "blk", 1.0 / 256), ("mL", "mN", -1.0 / UNIT), ("mR", "mI", 128.0), ("mO2", "t3", 2.0 ** 23), ("fB", "blk", -1.0),
+                ("mW", "mN", -128.0 / UNIT), ("fL", "mN", 128.0 / UNIT), ("mF", "t0", 2.0 ** 26), ("wX", "wW", 16.0 / W)))
+        ts(col(X8), col(XC), -1.0, -8.0, mul, add, ["xc"], ["x8"])
+        ts(col(OM), col(R15), 16.0, -1.0, mul, add, ["r15"], ["om"])
+        ts(col(G31), col(G16), 31.0, None, add, None, ["g16"], ["g31"])
+        act(T.t4[:], T.ji[:, 0:32], ACT.Abs, ["ji", "x8"], ["t4"], bias=col(X8))
+        ts(T.t5[:], T.blk[:], -2.0 ** 26, None, mul, None, ["blk"], ["t5"])
+        ts(T.mA[:], T.mI[:], 2.0 ** 27, None, mul, None, ["mI"], ["mA"])
+        ts(T.wK[:], T.ji[:], col(G15), col(OM), eq, mul, ["ji", "g15", "om"], ["wK"])
+        ts(T.w0[:], T.ji[:], col(G31), col(OM), eq, mul, ["ji", "g31", "om"], ["w0"])
         ts(T.OH[:], T.t4[:], 8.0, None, eq, None, ["t4"], ["OH"])
-        ts(T.ON[:], T.t4[:], 8.0, -128.0, ALU.not_equal, mul, ["t4"], ["ON"])
+        cp(T.ti[:], T.um[:], ["um"], ["ti"])
+        tt(T.mA[:], T.mA[:], T.t5[:], add, ["mA", "t5"], ["mA"])
+        tt(T.wK[:], T.wK[:], T.w0[:], add, ["wK", "w0"], ["wK"])
+        ts(T.ti[:], T.ti[:], 159, None, ALU.bitwise_and, None, ["ti"], ["ti"])
+        ts(T.t1[:], T.ti[:], 0.0, None, eq, None, ["ti"], ["t1"])
+        ts(T.t2[:], T.ti[:], 16.0, -1.0, eq, mul, ["ti"], ["t2"])
+        tt(T.mT[:], T.t1[:], T.t2[:], add, ["t1", "t2"], ["mT"])
 
-    def send(dst, out, src, sem, rd):
-        es = topo.engines(core, dst)
-        rid, pid = topo.addr(dst, core)
-        sent[0] += len(es)
+    def share(src, dst, part, parts):
+        es = topo.engines(src, dst)
+        if parts > 1: es = [e for e in es if all(e in topo.engines(src, c) for c in T.cores if c != src)]
+        return es[part * len(es) // parts:(part + 1) * len(es) // parts]
+
+    def send(items, rd):
+        trs = []
+        for j, (dst, out, srcs, sem) in enumerate(items):
+            es = share(core, dst, j, len(items))
+            rid, pid = topo.addr(dst, core)
+            sent[0] += len(es)
+            trs.append(RemoteDMATransfer(dst_ids=[DstId(rid=rid, pnc=pid)], dma_engine_mask=sum(1 << e for e in es), remote_sem=T.sem[sem],
+                                         srcs=srcs, dsts=[out], alu_op=1 if len(srcs) > 1 else 0))
         def call():
-            g.remote_dma(out, src, T.sem[sem], T.sem.sent, pid, rid, topo.mask(core, dst))
+            g.remote_dma_fused(trs, local_sem=T.sem.sent)
         op("G", call, rd, [], done=("sent", 0))
 
     def send_n(t):
-        if t in (2, 3):
-            dst, frm = (prv, nxt) if t == 2 else (opp, opp)
-            send(dst, lst(T.HI, t - 2), lst(T.NL, t), "ah%d" % (t - 2), ["NL%dA" % t, "NL%dB" % t])
-            arrives("ah%d" % (t - 2), len(topo.engines(frm, core)), ["HI%d" % (t - 2)])
+        items = [(nxt, lst(T.NI, t), [nlst(t)], "an%d" % t)]
+        if t in (2, 3): items.append((prv if t == 2 else opp, lst(T.HI, t - 2), [nlst(t)], "ah%d" % t))
+        send(items, ["NL%dA" % t, "NL%dB" % t])
+        arrives("an%d" % t, len(share(prv, core, 0, len(items))), ["NI%d" % t])
+        if t in (2, 3): arrives("ah%d" % t, len(share(nxt if t == 2 else opp, core, 1, 2)), ["HI%d" % (t - 2)])
 
     ne = len(topo.engines(prv, core))
-    win = T.Q[:, 0:W]
     X, Y, Z, U = (0, 1), (2, 3), (4, 5), (6, 7)
 
     def steps(t):
-        ni, mi = "NI%d" % t, "mi%d" % t
+        ni = "NI%d" % t
         last = t == TK - 1
         st = {}
-        def ms(buf, a, b): return buf[:, t * 2 * C + a:t * 2 * C + b]
 
         def half(h):
             k = "AB"[h]
             nl = "NL%d" % t + k
             sl, x, y, z, u = hs(h), X[h], Y[h], Z[h], U[h]
-            r0 = t * RW + 2 * C + h * H
-            qs, rs, ri = T.q1[:, sl], T.RS[:, r0:r0 + H], T.RI[:, r0:r0 + H]
-            kq, kr, ki = "q1" + k, "rs%d" % t + k, "ri%d" % t + k
-            hi, lo = [T.RS[:, (t + 1) * RW + a + 18 * h:(t + 1) * RW + a + 18 * h + 18] for a in (0, C)]
-            own, inc = lst(T.NL, t, 18 * h, 18 * h + 18), lst(T.NI, t, 18 * h, 18 * h + 18)
+            xh, yh, zh, uh, xl, yl, ul = (x, "h"), (y, "h"), (z, "h"), (u, "h"), (x, "l"), (y, "l"), (u, "l")
+            tl = slice(t * R + h * H, t * R + (h + 1) * H)
+            qs, ps, fs, rs, mn = T.q1[:, tl], T.p1[:, tl], T.fo1[:, tl], T.rr[:, sl], T.mn[:, sl]
+            kq, kp, kf, kd, ki, kr, km = ["%s%d%s" % (s, t, k) for s in ("q1", "p1", "fo1", "di", "fi")] + ["rr" + k, "mn" + k]
+            own, inc = nlst(t, 18 * h, 18 * h + 18), lst(T.NI, t, 18 * h, 18 * h + 18)
             ls = slice(18 * h, 18 * h + 18)
-            of1, nb = T.OF1[:, ls], bank(y)[:, H + 64:H + 82]
-            def tx():
-                a = t * RW if h == 0 else r0
-                rd = [kr] + (["hi%dA" % t, "hi%dB" % t, "lo%dA" % t, "lo%dB" % t] if h == 0 else [])
-                send(nxt, T.RI[:, a:r0 + H], T.RS[:, a:r0 + H], "a%s%d" % ("ab"[h], t), rd)
-                arrives("a%s%d" % ("ab"[h], t), ne, [ki])
-            def dl():
-                mm(u, bh(u), T.mP[:], T.p1[:, sl], True, False, ["mP", "p1" + k])
-                mm(u, bh(u), T.mM[:], qs, False, True, ["mM", kq])
-            def qq():
-                if h == 0 and k not in FB: cp(T.q2[:, sl], win.indirect(inc), ["Q", ni], ["q2" + k])
-                else: act(T.q2[:, sl], win.indirect(inc), Ident, ["Q", ni], ["q2" + k])
-            def sq():
-                if k in FB: tt(T.sq[:, sl], win.indirect(inc), T.sb[:, sl], mul, ["Q", ni, "sb" + k], ["sq" + k])
-                else: tt(T.sq[:, sl], T.q2[:, sl], bh(y), mul, ["q2" + k], ["sq" + k], [y])
-            def sgm():
-                mm(z, bl(z, 18), T.mS[:], T.VL[:, ls], True, True, ["mS", "vl" + k])
-                mm(y, nb, T.mI[:], T.VL[:, ls], True, False, ["mI", "vl" + k])
-            def oe():
-                mm(u, bh(u), T.mI[:], T.ec[:, sl], True, False, ["mI", "ec"])
-                mm(u, bh(u), T.mI[:], T.og[:, sl], False, True, ["mI", "og" + k])
+            of1 = T.OF1[:, ls]
+            ub = [T.UB[:, (2 * t + j) * R + h * H:(2 * t + j) * R + (h + 1) * H] for j in (0, 1)]
+            def lanes(name, land, srcs):
+                ks = "AB" if name in WHOLE else k
+                if ks[-1] != k: return
+                a = slice(t * R, (t + 1) * R) if name in WHOLE else tl
+                send([(nxt, T[land][:, a], [T[s][:, a] for s in srcs], "%s%s%d" % (name, k, t))],
+                     ["%s%d%s" % (s, t, j) for s in srcs for j in ks])
+                arrives("%s%s%d" % (name, k, t), ne, ["%si%d%s" % (name, t, j) for j in ks])
+            def tx(): lanes("d", "DI", ["p1", "q1"])
+            def tf(): lanes("f", "FI", ["fo1"])
+            def gq():
+                if t == 0: scale_to("gq" + k, qs, T.Q0[:].indirect(own), -1.0 / UNIT, ["Q0", nl], [kq])
+                else: scale_to("gq" + k, qs, T.Q[:, 0:W].indirect(own), -1.0, ["Q", nl], [kq])
+            def rr():
+                if "rr" + k in ONV: ts(rs, T.DI[:, tl], 0.0, 256.0 * UNIT, ALU.max, mul, [kd], [kr])
+                else: act(rs, T.DI[:, tl], Relu, [kd], [kr], scale=256.0 * UNIT)
             d = {
                 "a": lambda: uni(x, "sN", "UD", 2 * t, h, False),
-                "c": lambda: uni(y, "sC", "UA", 3 * t, h, True),
-                "p": lambda: mm(u, bl(u, 18), T.fI[:], T.sp1[:, t * C + 18 * h:t * C + 18 * h + 18], True, False, ["fI", "sp1"]),
-                "gq": lambda: cp(qs, win.indirect(own), ["Q", nl], [kq]),
-                "gp": lambda: act(T.p1[:, sl], T.P[:].indirect(own), Ident, ["P", nl], ["p1" + k]),
-                "dl": dl,
-                "rl": lambda: act(rs, bh(u), Relu, [], [kr], [u]),
-                "tx": tx,
-                "Lq": lambda: mm(x, bh(x), T.mL[:], qs, False, True, ["mL", kq]),
-                "Ip": lambda: mm(z, bh(z), T.mI[:], T.p1[:, sl], True, False, ["mI", "p1" + k]),
-                "sg": lambda: act(T.s1[:, sl], bh(x), Sign, [], ["s1" + k], [x], bias=-0.5),
-                "cq": lambda: tt(T.cq[:, sl], qs, bh(y), mul, [kq], ["cq" + k], [y]),
-                "pm": lambda: mm(z, bh(z), T.mO1[:], T.s1[:, sl], False, True, ["mO1", "s1" + k]),
-                "f": lambda: tt(T.fo1[:, sl], T.cq[:, sl], bh(z), ALU.is_lt, ["cq" + k], ["fo1" + k], [z]),
-                "cv": lambda: conv(u, bl(u, 18), "wW", "fo1", h * H, H, False, True, ["fo1" + k]),
-                "of": lambda: cp(of1, bl(u, 18), [], ["of1" + k], [u]),
-                "x1": lambda: cp(T.Q[:, 0:2 * W].indirect(of1), T.p1[:, sl], ["of1" + k, "p1" + k], ["Q"]),
-                "g2": lambda: act(T.p2[:, sl], T.P[:].indirect(inc), Ident, ["P", ni], ["p2" + k]),
+                "c": lambda: uni(y, "sC", "UC", 3 * t, h, True),
+                "p": lambda: mm(ul, bl(u, 18), T.hI[:], T.sph[:, t * C + 18 * h:t * C + 18 * h + 18], True, False, ["hI", "sph"]),
+                "gq": gq,
+                "gp": lambda: scale_to("gp" + k, ps, T.P[:].indirect(own), 1.0 / UNIT, ["P", nl], [kp]),
+                "tx": tx, "tf": tf,
+                "Lq": lambda: mm(xh, bh(x), T.mN[:], qs, False, True, ["mN", kq]),
+                "Ip": lambda: mm(zh, bh(z), T.mP[:], ps, True, False, ["mP", kp]),
+                "sg": lambda: act(T.s1[:, sl], bh(x), Sign, [xh], ["s1" + k], bias=-0.5),
+                "cq": lambda: tt(T.cq[:, sl], qs, bh(y), mul, [kq, yh], ["cq" + k]),
+                "pm": lambda: mm(zh, bh(z), T.mO1[:], T.s1[:, sl], False, True, ["mO1", "s1" + k]),
+                "f": lambda: tt(fs, T.cq[:, sl], bh(z), ALU.is_lt, ["cq" + k, zh], [kf]),
+                "cv": lambda: conv(ul, bl(u, 18), "wW", "fo1", t * R + h * H, H, False, True, [kf]),
+                "of": lambda: cp(of1, bl(u, 18), [ul], ["of1" + k]),
+                "x1": lambda: cp(T.Q[:].indirect(of1), ps, ["of1" + k, kp], ["Q"]),
+                "rr": rr,
                 "b": lambda: uni(z, "sN", "UD", 2 * t + 1, h, False),
-                "d": lambda: uni(u, "sC", "UA", 3 * t + 1, h, True),
-                "e": lambda: uni(y, "sE", "UA", 3 * t + 2, h, True),
-                "S": lambda: mm(y, bh(y), T.mB[:], ri, True, True, ["mB", ki]),
-                "Ir": lambda: mm(x, bh(x), T.mI[:], ri, True, True, ["mI", ki]),
-                "qq": qq, "sq": sq,
-                "L2": lambda: mm(z, bh(z), T.mL[:], T.q2[:, sl], False, True, ["mL", "q2" + k]),
-                "s2": lambda: act(T.s2[:, sl], bh(z), Sign, [], ["s2" + k], [z], bias=-0.5),
-                "wr": lambda: tt(T.wr[:, sl], bh(x), T.sq[:, sl], sub, ["sq" + k], ["wr" + k], [x]),
-                "rw": lambda: act(T.wp[:, sl], T.wr[:, sl], Relu, ["wr" + k], ["wp" + k]),
-                "I2": lambda: mm(x, bh(x), T.mI[:], ri, True, False, ["mI", ki]),
-                "p2": lambda: mm(x, bh(x), T.mO2[:], T.s2[:, sl], False, True, ["mO2", "s2" + k]),
-                "Lw": lambda: mm(z, bh(z), T.fL[:], T.wp[:, sl], True, False, ["fL", "wp" + k]),
-                "dq": lambda: tt(T.dq[:, sl], T.sq[:, sl], bh(u), mul, ["sq" + k], ["dq" + k], [u]),
-                "f2": lambda: tt(T.fo2[:, sl], T.dq[:, sl], bh(x), ALU.is_lt, ["dq" + k], ["fo2" + k], [x]),
-                "ew": lambda: tt(T.ew[:, sl], T.wp[:, sl], bh(y), mul, ["wp" + k], ["ew" + k], [y]),
-                "Ow": lambda: mm(z, bh(z), T.fB[:], T.ew[:, sl], False, False, ["fB", "ew" + k]),
-                "ov": lambda: mm(z, bh(z), T.mF[:], T.fo2[:, sl], False, True, ["mF", "fo2" + k]),
-                "sv": lambda: act(T.sv[:, sl], bh(z), Sign, [], ["sv" + k], [z], bias=-0.5),
-                "vp": lambda: mm(y, bl(y, 18), T.mG[:], ms(T.MI, C + 18 * h, C + 18 * h + 18), True, False, ["mG", mi]),
-                "cvv": lambda: conv(y, bl(y, 18), "wU", "sv", h * H, H, False, True, ["sv" + k]),
-                "vmx": lambda: tt(T.VL[:, ls], bl(y, 18), ms(T.MI, 18 * h, 18 * h + 18), ALU.max, [mi], ["vl" + k], [y]),
-                "sgm": sgm,
-                "sgc": lambda: cp(T.SG[:, ls], bl(z, 18), [], ["sg" + k], [z]),
-                "cve": lambda: conv(y, nb, "wX", "eo", h * H, H, False, True, ["eo" + k]),
-                "nl": lambda: cp(lst(T.NL, t + 1, 18 * h, 18 * h + 18), nb, [], ["NL%d" % (t + 1) + k], [y]),
-                "yn": lambda: act(T.YN[:, t * C + 18 * h:t * C + 18 * h + 18], nb, Ident, [], ["yn%d" % t + k], [y]),
-                "hi": lambda: act(hi, nb, Ident, [], ["hi%d" % (t + 1) + k], [y]),
-                "lo": lambda: tt(lo, nb, hi, sub, ["hi%d" % (t + 1) + k], ["lo%d" % (t + 1) + k], [y]),
+                "S": lambda: mm(yh, bh(y), T.mB[:], rs, True, True, ["mB", kr]),
+                "qq": lambda: scale_to("qq" + k, T.q2[:, sl], T.Q[:, 0:W].indirect(inc), UNIT, ["Q", ni], ["q2" + k]),
+                "sq": lambda: tt(bh(y), T.q2[:, sl], bh(y), mul, ["q2" + k, yh], [yh]),
+                "L2": lambda: mm(zh, bh(z), T.mL[:], T.q2[:, sl], False, True, ["mL", "q2" + k]),
+                "s2": lambda: act(T.s2[:, sl], bh(z), Sign, [zh], ["s2" + k], bias=-0.5),
+                "I2": lambda: mm(xh, bh(x), T.mR[:], rs, True, False, ["mR", kr]),
+                "A": lambda: mm(xh, bh(x), T.mA[:], T.FI[:, tl], False, False, ["mA", ki]),
+                "p2": lambda: mm(xh, bh(x), T.mO2[:], T.s2[:, sl], False, True, ["mO2", "s2" + k]),
+                "dq": lambda: tt(T.dq[:, sl], ub[0], bh(y), mul, ["ub%d" % t, yh], ["dq" + k]),
+                "f2": lambda: tt(T.fo2[:, sl], T.dq[:, sl], bh(x), ALU.is_lt, ["dq" + k, xh], ["fo2" + k]),
+                "mn": lambda: tt(mn, rs, bh(y), ALU.min, [kr, yh], [km]),
+                "Br": lambda: mm(uh, bh(u), T.blk[:], rs, True, False, ["blk", kr]),
+                "Bm": lambda: mm(uh, bh(u), T.fB[:], mn, False, True, ["fB", km]),
+                "Lr": lambda: mm(zh, bh(z), T.mW[:], rs, True, False, ["mW", kr]),
+                "Lm": lambda: mm(zh, bh(z), T.fL[:], mn, False, False, ["fL", km]),
+                "ov": lambda: mm(zh, bh(z), T.mF[:], T.fo2[:, sl], False, True, ["mF", "fo2" + k]),
+                "t": lambda: tt(T.th[:, sl], ub[1], bh(u), mul, ["ub%d" % t, uh], ["th" + k]),
+                "sv": lambda: tt(T.sv[:, sl], T.th[:, sl], bh(z), ALU.is_lt, ["th" + k, zh], ["sv" + k]),
+                "cvk": lambda: conv(yl, bl(y, 18), "wK", "sv", h * H, H, True, True, ["sv" + k]),
+                "sgc": lambda: cp(T.SG[:, ls], bl(y, 18), [yl], ["sg" + k]),
+                "kb": lambda: act(T.KB[:, ls], bl(y, 18), Ident, [yl], ["kb" + k]),
+                "alt": lambda: mm(xl, bl(x, 18), T.mT[:], T.KB[:, ls], True, False, ["mT", "kb" + k]),
+                "eo": lambda: tt(T.eo[:, sl], T.OH[:].indirect(T.SG[:, ls]), T.ec[:, sl], mul, ["OH", "sg" + k, "ec"], ["eo" + k]),
+                "cve": lambda: conv(xl, bl(x, 18), "wX", "eo", h * H, H, False, True, ["eo" + k]),
+                "nl": lambda: cp(nlst(t + 1, 18 * h, 18 * h + 18), bl(x, 18), [xl], ["NL%d" % (t + 1) + k]),
             }
-            if k in FB: d["Sc"] = lambda: act(T.sb[:, sl], bh(y), Ident, [], ["sb" + k], [y])
-            if k in FD and not last:
-                d["og"] = lambda: act(T.og[:, sl], T.ON[:].indirect(T.SG[:, ls]), Ident, ["ON", "sg" + k], ["og" + k])
-                d["oe"] = oe
-                d["or"] = lambda: act(T.eo[:, sl], bh(u), Relu, [], ["eo" + k], [u])
-            else:
-                d["eo"] = lambda: tt(T.eo[:, sl], T.OH[:].indirect(T.SG[:, ls]), T.ec[:, sl], mul, ["OH", "sg" + k, "ec"], ["eo" + k])
             if last:
+                d["yn"] = lambda: act(T.YN[:, t * C + 18 * h:t * C + 18 * h + 18], bl(x, 18), Ident, [xl], ["yn" + k])
                 d["k"] = lambda: tt(T.hx[:, sl], T.F[:].indirect(inc), T.hh[:, sl], add, ["F", ni, "hh" + k], ["hx" + k])
                 d["tk"] = lambda: act(T.hh[:, sl], T.hx[:, sl], Tanh, ["hx" + k], ["hh" + k])
             for name in d:
@@ -336,68 +355,58 @@ def rank_program(g, core, T, topo):
         half(0)
         half(1)
 
-        def msg():
-            act(ms(T.MS, 0, C), bl(Y[0]), Ident, [], ["msa%d" % t], [Y[0]], bias=-16.0)
-            act(ms(T.MS, C, 2 * C), bl(Y[0]), Sign, [], ["msb%d" % t], [Y[0]], bias=-15.5)
-            send(nxt, ms(T.MI, 0, 2 * C), ms(T.MS, 0, 2 * C), "am%d" % t, ["msa%d" % t, "msb%d" % t])
-            arrives("am%d" % t, ne, [mi])
-        def nm():
-            mm(X[0], bl(X[0]), T.mI[:], T.RI[:, t * RW:t * RW + C], True, False, ["mI", "ri%dA" % t])
-            mm(X[0], bl(X[0]), T.mI[:], T.RI[:, t * RW + C:t * RW + 2 * C], False, True, ["mI", "ri%dA" % t])
-        def o2c():
-            conv(U[0], bl(U[0]), "wW", "fo2", 0, R, False, False, ["fo2A", "fo2B"])
-            mm(U[0], bl(U[0]), T.mH[:], ms(T.MI, C, 2 * C), False, True, ["mH", mi])
+        ol, oa = (Y[1], "o"), bl(Y[1], C, 32)
         def x2(j):
             a, b = X2CUT[j], X2CUT[j + 1]
-            if b > a: cp(T.Q[:].indirect(T.OF2[:, a:b]), T.p2[:, 16 * a:16 * b], ["of2", "p2A", "p2B"], ["Q"])
-        fo1, hh, hx = ["fo1A"], ["hhA", "hhB"], ["hxA", "hxB"]
+            if b > a: op("S", lambda: S.activation(T.Q[:].indirect(T.OF2[:, a:b]), T.p2[:, 16 * a:16 * b], Tanh), ["of2", "p2"], ["Q"])
+        hh, hx = ["hhA", "hhB"], ["hxA", "hxB"]
         st.update({
-            "sn": lambda: send_n(t),
-            "c1a": lambda: conv(U[0], bl(U[0], 18), "wW", "fo1", 0, H, False, True, fo1, range(0, 6)),
-            "c1b": lambda: conv(U[0], bl(U[0], 18), "wW", "fo1", 0, H, False, True, fo1, range(6, 16)),
-            "cd1": lambda: conv(Y[0], bl(Y[0]), "wV", "s1", 0, R, True, False, ["s1A", "s1B"]),
-            "cd2": lambda: conv(Y[0], bl(Y[0]), "wX", "fo1", 0, R, False, True, ["fo1A", "fo1B"]),
-            "msg": msg, "nm": nm,
-            "nc": lambda: cp(lst(T.NI, t), bl(X[0]), [], [ni], [X[0]]),
-            "ecg": lambda: act(T.ec[:], T.E[:].indirect(lst(T.NI, t)), Ident, ["E", ni], ["ec"]),
-            "o2p": lambda: mm(U[0], bl(U[0]), T.fI[:], T.sp2[:, t * C:(t + 1) * C], True, False, ["fI", "sp2"]),
-            "o2c": o2c,
-            "of2": lambda: cp(T.OF2[:, 0:C], bl(U[0]), [], ["of2"], [U[0]]),
-            "x2a": lambda: x2(0), "x2b": lambda: x2(1), "x2c": lambda: x2(2),
+            "sn": lambda: send_n(t), "bc": lambda: spread(t),
+            "ecg": lambda: scale_to("ecg", T.ec[:], T.E[:].indirect(lst(T.NI, t)), 1.0, ["E", ni], ["ec"]),
         })
+        if not last:
+            st.update({
+                "g2": lambda: scale_to("g2", T.p2[:], T.P[:].indirect(lst(T.NI, t)), 1.0 / UNIT, ["P", ni], ["p2"]),
+                "o2p": lambda: mm(ol, oa, T.hI[:], T.sph[:, t * C:(t + 1) * C], True, False, ["hI", "sph"]),
+                "o2c": lambda: conv(ol, oa, "wW", "fo2", 0, R, False, True, ["fo2A", "fo2B"]),
+                "of2": lambda: cp(T.OF2[:], oa, [ol], ["of2"]),
+                "x2a": lambda: x2(0), "x2b": lambda: x2(1), "x2c": lambda: x2(2),
+            })
         if t == 1:
-            st["th"] = lambda: act(T.hh[:], T.F[:].indirect(lst(T.NL, 1)), Tanh, ["F", "NL1A", "NL1B"], hh)
+            st["th"] = lambda: act(T.hh[:], T.F[:].indirect(nlst(1)), Tanh, ["F", "NL1A", "NL1B"], hh)
         if t in (2, 3):
             st["hg"] = lambda: act(T.hx[:], T.F[:].indirect(lst(T.HI, t - 2)), Ident, ["F", "HI%d" % (t - 2)], hx)
             st["hd"] = lambda: op("G", lambda: g.dma_start(T.hh[:], T.hx[:], accum_op=add), hx + hh, hh, done=("hd%d" % t, 16))
         if t in (3, 4):
             st["th"] = lambda: act(T.hh[:], T.hh[:], Tanh, hh, hh)
         if last:
-            for name in ("o2p", "o2c", "of2", "x2a", "x2b", "x2c", "hiA", "hiB", "loA", "loB", "g2A", "g2B"):
-                del st[name]
+            st["yn"] = lambda: cp(T.YN[:, 0:t * C], T.NL[:, C:TK * C], ["NL%d%s" % (j, k) for j in range(1, TK) for k in "AB"], ["yn"])
         return st
 
     def out_h(k, a, b):
         sl = slice(16 * a, 16 * b)
-        tt(T.hx[:, sl], T.F[:].indirect(lst(T.NL, TK, a, b)), T.hh[:, sl], add, ["F", "NL%d" % TK + k, "hh" + k], ["hz%d" % a])
-        act(T.wr[:, sl], T.hx[:, sl], Tanh, ["hz%d" % a], ["ho%d" % a, "wr" + k])
-        op("Y", lambda: g.sync.dma_start(T.yh[:, sl], T.wr[:, sl]), ["ho%d" % a], [], done=("stored", 16))
+        tt(T.hx[:, sl], T.F[:].indirect(nlst(TK, a, b)), T.hh[:, sl], add, ["F", "NL%d" % TK + k, "hh" + k], ["hz%d" % a, "hx" + k])
+        act(T.ho[:, sl], T.hx[:, sl], Tanh, ["hz%d" % a], ["ho%d" % a])
+        op("Y", lambda: g.sync.dma_start(T.yh[:, sl], T.ho[:, sl]), ["ho%d" % a], [], done=("stored", 16))
 
     def out_b():
-        op("Y", lambda: g.sync.dma_start(T.yn[:], T.YN[:]), ["yn%d%s" % (t, k) for t in range(TK) for k in "AB"], [],
-           done=("stored", 16))
         for a, b in zip(TAIL, TAIL[1:]): out_h("B", a, b)
 
-    every = [steps(t) for t in range(TK)] + [{"gqA": lambda: out_h("A", 0, 18), "gqB": out_b}]
-    every[0]["spc"] = lambda: cp(T.sp1[:], T.spi[:], ["spi"], ["sp1"])
-    every[0]["spd"] = lambda: ts(T.sp2[:], T.sp1[:], W / 2.0, None, add, None, ["sp1"], ["sp2"])
-    every[0]["late"] = late
-    for name in FIRST:
-        every[0][name]()
-    for t in range(TK):
-        for name in ORDER:
-            st = every[t + 1] if name[0] == "+" else every[t]
-            if name.lstrip("+") in st: st[name.lstrip("+")]()
+    def out_n():
+        op("S", lambda: g.scalar.dma_start(T.yn[:], T.YN[:]), ["yn", "ynA", "ynB"], [], done=("stored", 16))
+
+    def places():
+        cp(T.sp1[:], T.spi[:], ["spi"], ["sp1"])
+        cp(T.sph[:], T.sp1[:], ["sp1"], ["sph"])
+
+    every = [steps(t) for t in range(TK)] + [{"gqA": lambda: out_h("A", 0, 18), "gqB": out_b, "sn": out_n}]
+    every[0].update({"spc": places, "late": late,
+                     "qf": lambda: ts(T.Q[:, 0:W], T.Q0[:], 1.0 / UNIT, None, mul, None, ["Q0"], ["Q"])})
+    for t, names in [(0, FIRST)] + [(t, ORDER) for t in range(TK - 1)] + [(TK - 1, LAST)]:
+        for name in names:
+            u = t + 1 if name[0] == "+" else t
+            now[0] = name.lstrip("+") + str(u)
+            if name.lstrip("+") in every[u]: every[u][name.lstrip("+")]()
     final.append(("stored", 16 * (len(TAIL) + 1)))
     final.append(("sent", sent[0]))
     emit(g, T, ops, final)

@@ -2,7 +2,8 @@ from concourse.bass import DstId, RemoteDMATransfer
 from concourse.mybir import AluOpType as ALU, ActivationFunctionType as ACT
 
 W, R, TK, C = 1280, 576, 5, 36
-H = R // 2
+CUT = [0, 18, 36]
+LB = 352
 LS = 40
 UNIT = 4096.0
 
@@ -15,10 +16,15 @@ SCRATCH = {
     "sp1": ("sbuf", [128, TK * C], "float32"), "sph": ("sbuf", [128, TK * C], "float16"),
     "NL": ("sbuf", [128, (TK + 1) * C], "uint16"), "NI": ("sbuf", [128, TK * LS], "uint16"),
     "HI": ("sbuf", [128, 2 * LS], "uint16"),
-    "KB": ("sbuf", [128, C], "bfloat16"), "OF1": ("sbuf", [128, C], "uint16"), "OF2": ("sbuf", [128, C], "uint16"),
+    "OF1": ("sbuf", [128, C], "uint16"), "OF2": ("sbuf", [128, C], "uint16"),
     "SG": ("sbuf", [128, C], "uint16"), "YN": ("sbuf", [128, TK * C], "float32"),
-    "ji": ("sbuf", [128, 144], "bfloat16"), "pi": ("sbuf", [128, 4], "int32"), "col": ("sbuf", [128, 16], "bfloat16"),
-    "OH": ("sbuf", [128, 32], "bfloat16"), "t4": ("sbuf", [128, 32], "bfloat16"), "hI": ("sbuf", [128, 128], "float16"),
+    "pi": ("sbuf", [128, 4], "int32"), "col": ("sbuf", [128, 16], "bfloat16"), "ti": ("sbuf", [128, 32], "int32"),
+    "OH": ("sbuf", [128, 32], "bfloat16"), "hI": ("sbuf", [128, 128], "float16"),
+    "ji": ("sbuf", [128, 144], "bfloat16"), "wW": ("sbuf", [128, 144], "bfloat16"), "wX": ("sbuf", [128, 144], "bfloat16"),
+    "wK": ("sbuf", [128, 144], "bfloat16"), "w0": ("sbuf", [128, 144], "bfloat16"), "KB": ("sbuf", [128, C], "bfloat16"),
+    "mT": ("sbuf", [128, 128], "bfloat16"), "tj": ("sbuf", [128, 128], "int32"),
+    "gB": ("sbuf", [128, 8], "bfloat16"), "gK": ("sbuf", [128, 24], "bfloat16"),
+    "wI": ("sbuf", [128, C], "bfloat16"), "xI": ("sbuf", [128, C], "bfloat16"), "TT": ("sbuf", [128, 10 * 128], "bfloat16"),
 }
 for _n in ("p1", "q1", "fo1", "DI", "FI"):
     SCRATCH[_n] = ("sbuf", [128, TK * R], "bfloat16")
@@ -26,14 +32,11 @@ for _n in ("s1", "rr", "q2", "s2", "fo2", "sv", "ec", "eo"):
     SCRATCH[_n] = ("sbuf", [128, R], "bfloat16")
 for _n in ("cq", "p2", "mn", "th", "dq", "hh", "hx", "ho"):
     SCRATCH[_n] = ("sbuf", [128, R], "float32")
-for _n in ("mL", "mN", "mI", "mP", "mR", "mW", "mO1", "mO2", "mB", "mF", "mA", "mT", "sN", "sC",
-           "um", "gm", "blk", "t0", "t1", "t2", "t3", "t5"):
+for _n in ("mL", "mN", "mI", "mP", "mR", "mW", "mO1", "mO2", "mB", "mF", "mA", "sN", "sC",
+           "um", "gm", "blk", "t0", "t1", "t2", "t3", "t4", "t5"):
     SCRATCH[_n] = ("sbuf", [128, 128], "bfloat16")
 for _n in ("fL", "fB"):
     SCRATCH[_n] = ("sbuf", [128, 128], "float32")
-for _n in ("wK", "wW", "wX", "w0"):
-    SCRATCH[_n] = ("sbuf", [128, 144], "bfloat16")
-SCRATCH["ti"] = ("sbuf", [128, 128], "int32")
 for _i in range(8):
     SCRATCH["b%d" % _i] = ("psum", [128, 512], "float32")
 
@@ -41,19 +44,39 @@ LOADS = ["n0", "qd", "pt", "ud", "ue", "ua", "ub", "spot", "nx", "vf"]
 SEMAPHORES = (["cV", "cS", "cP", "cG", "sent", "stored", "ah2", "ah3", "hd2", "hd3"] + ["ld_" + n for n in LOADS]
               + ["%s%d" % (k, t) for t in range(TK) for k in ("an", "dA", "dB", "fA", "fB", "ub")])
 
-ONV = ["gqA", "qqB", "rrA", "rrB"]
-WHOLE = ""
-X2CUT = [0, 12, 24, 36]
-TAIL = [18, 28, 36]
-FIRST = """bc aA aB cA cB gpA gqA sn IpA gqB cqA LqA LqB sgA gpB spc qf pA pB pmA IpB fA cqB txA txB sgB pmB late fB tfA tfB cvA bA ofA x1A""".split()
-ORDER = """cvB ofB th x1B rrA rrB SA SB BrA BrB I2A AA hg ecg g2 qqA qqB bB L2A sqA s2A mnA dqA hd L2B sqB s2B p2A LrA BmA f2A mnB I2B AB p2B dqB
-LmA f2B ovA o2p o2c tA svA of2 LrB BmB LmB ovB cvkA x2a kA tB svB sgcA kbA eoA altA cvkB x2b kB tkA cveA sgcB kbB eoB altB nlA x2c tkB cveB nlB
-yn +bc +sn +aA +aB +cA +cB +gpA +gqA +gqB +txA +pA +LqA +sgA +IpA +LqB +gpB +pmA +cqA +cqB +txB +sgB +fA +tfA +IpB +pmB +cvA +fB +tfB +ofA
-+x1A +bA +pB""".split()
 ONV = ["gpA", "gqB", "qqB"]
-FIRST = """aA qf gpB gqA gqB cB aB cA IpB sn LqB LqA spc gpA txA cqA IpA cqB kA sgA txB pmA pB fA pA sgB pmB fB late th bA rrA cvA cvB bB ofB rrB SA BrB ofA x1A BrA I2A x1B qqA L2A qqB sqA s2A SB L2B""".split()
-ORDER = """kB I2B o2p mnA LrA bc s2B BmA tfA ecg sqB hg LrB mnB BmB dqB AA dqA tfB tB p2A AB p2B f2A f2B tA LmA ovA svA g2 o2c cvkA of2 x2a LmB sgcA kbA x2b ovB svB cvkB eoA sgcB eoB x2c hd altA kbB cveA altB cveB nlA +gqA +cB +aA +gpA nlB +gpB +cA +LqA +txA tkA +gqB +sgA +IpA +cqA +aB +LqB +cqB +sgB +pmA +fA +IpB +sn +pmB +rrA +fB +txB tkB +pA +pB +yn +cvA ynB +ofA +x1A +cvB +I2A +SA +ofB +x1B +th +bA +kA +qqA +bB +BrA +qqB +rrB +L2A +L2B +s2A +SB +BrB +sqA ynA""".split()
-LAST = """I2B bc tfA ecg s2B LrA mnA sqB dqA BmA tA mnB LmA LrB dqB AA p2A BmB f2A tfB kB AB p2B f2B ovA LmB svA ovB tB svB cvkA sgcA cvkB eoA kbA tkB kbB sgcB altA eoB cveA altB tkA nlA cveB +gqA nlB ynB ynA +sn +gqB""".split()
+WHOLE = ""
+TURN = []
+WIDE = True
+SPLIT = ""
+BOTH = ""
+LDKEY = "go0"
+FEW = True
+TAIL = [10, 28]
+FIRST = """m1 m2 m3 m4 m5 m6 bc sn aA aB cA cB gpA gqA gqB LqA IpA gpB txA cqA sgA LqB IpB txB spc qf pmA cqB sgB fA pmB cvA evA cwA tfA fB tfB cvB evB cwB
+ofA x1A rrA rrB th bA bB SA SB I2A I2B BrA BrB ofB g2 ecg x1B""".split()
+ORDER = """qqA qqB AA AB L2A sqA mnA L2B s2A s2B BmA sqB mnB p2A LrA LmA dqA f2A p2B dqB f2B ovA tA svA ocA oeA owA ogA ocB oeB owB ogB LrB BmB hg hd kA
+x2A cvkA ekA ckA tB LmB ovB svB sgcA kbA eoA y2A cvkB ekB ckB altA cveA eeA ceA kB tkA sgcB kbB eoB x2B y2B altB cveB eeB ceB nlA ynA tkB nlB ynB +bc
++sn +aA +aB +cA +cB +gpA +gqA +gqB +LqA +IpA +gpB +txA +cqA +sgA +LqB +IpB +txB +pmA +cqB +sgB +fA +pmB +cvA +evA +cwA +tfA +fB +tfB +cvB +evB
++cwB +ofA +x1A +rrA +rrB +th +yn +bA +bB +SA +SB +I2A +I2B +BrA +BrB +ofB +g2 +ecg +x1B""".split()
+FIRST = """aA m6 gqA qf sn m5 gqB gpB gpA aB LqA cA IpA LqB sgA sgB cB pmA spc cqA IpB txA fA cvA m2 cqB evA pmB cwA fB m3 cvB txB evB m1 ofA x1A m4 cwB rrA bB ofB SA x1B bA""".split()
+ORDER = """bc qqB tfA qqA L2A s2A rrB sqA mnA L2B BrA dqA tfB I2A LrA BmA s2B SB LmA AA hg p2A sqB I2B LrB mnB f2A tA BrB ovA svA BmB ecg ocA g2 cvkA oeA AB ekA dqB kbA tB p2B owA LmB ckA ogA f2B ocB x2A ovB oeB sgcA y2A eoA owB cveA svB altA +aA hd eeA ogB cvkB x2B ceA ekB y2B nlA +gqA +cA ckB +aB +gpA sgcB eoB cveB +cqA kbB eeB +LqA +sgA altB +IpA +txA ceB +cB +pmA nlB +gqB +gpB +fA +LqB +cqB +IpB +sn +sgB +txB +cvA +evA +pmB +fB +th +cwA +cvB +bA +bB +evB +ofA +cwB +x1A +rrA +ofB +x1B +SA""".split()
+LAST = """BrA qqA qqB L2A bc tfA s2A tfB L2B sqA I2A mnA kB LrA kA LmA dqA s2B rrB SB sqB mnB BmA BrB LrB tkB yn AA dqB p2A I2B BmB f2A AB p2B tB ecg LmB f2B ovB tA ovA svB cvkB tkA svA ekB cvkA kbA ekA ckB ckA sgcB eoB kbB sgcA cveB eeB eoA altB ceB nlB cveA eeA altA ceA ynB ynA +sn +gqB nlA +gqA""".split()
+ONV = ["gqA", "gqB", "qqB"]
+CUT = [0, 20, 36]
+FIRST = """bc m2 m1 m7 gqA m5 gqB aA aB cB cA LqA spc cqA gpA LqB gpB sgA sgB sn IpA cqB txA qf IpB pmA fA pmB fB cvB m4 cvA m3 cwA cwB txB rrA tfA ofA x1A ofB x1B qqA ld rrB bA SA bB m6 L2A qqB sqA L2B I2A mnA dqA SB s2A I2B AA LrA sqB dqB s2B BmA mnB p2A""".split()
+ORDER = """tfB ecg g2 f2A AB hd p2B ocB LmA f2B ovA owB tA LrB svA ogB ckA BmB LmB ovB x2A sgcA kbA eoA tB svB x2B altA ceA nlA ckB +cA +aA +aB +bc +gqA sgcB eoB +gpA +LqA kbB +sgA altB ceB +cvA +IpA +cqA nlB +pmA +cvB +gqB +txA +cB +fA +LqB +sn +gpB +yn +cqB +IpB +sgB +cwA +th +rrA +hg +pmB +ofA +fB +x1A +cwB +txB +ofB +x1B +SA +qqA +bA +I2A +bB +rrB +L2A +kB +qqB +L2B +s2A +SB +sqA +I2B +tfA +mnA +AA +sqB +dqA +mnB +dqB +p2A +s2B +LrA +BmA""".split()
+LAST = """tkB tA LrB tfB AB ecg p2B BmB LmB f2B ovB tB f2A svB LmA ovA ckB kA svA sgcB ckA eoB sgcA kbB tkA altB kbA eoA ceB altA ceA nlB +gqB nlA ynA ynB +sn +gqA""".split()
+FIRST = """m2 m7 gpB gqA m5 gqB gpA spc cB aA aB LqA LqB sn IpB IpA cA sgA sgB txA qf pmA cvA pmB cvB cqB cqA txB fA cwA m3 m1 tfA fB ofA bA cwB tfB x1A bc ofB rrA x1B qqA rrB SA BrA I2A bB L2A s2A m4 m6 qqB sqA SB I2B BrB L2B mnA sqB AA mnB p2A LrA s2B dqA ld""".split()
+ORDER = """hd BmA dqB f2A ecg AB p2B f2B LmA g2 ovA ocB owB LrB tA svA ogB x2A ckA BmB LmB sgcA eoA ovB kbA altA tB svB ceA nlA x2B +gpA +gqA ckB +aA +cA sgcB kbB +LqA +IpA +sgA +cvA altB eoB ceB +cqA nlB +pmA +cvB +cB +aB +txA +gqB +fA +cqB +LqB +gpB +sn +txB +IpB +bc +cwA +sgB +ofA +pmB +fB +th +x1A +cwB +rrA +hg +rrB +BrA +bA +SA +bB +ofB +tfA +BrB +x1B +kB +qqB +SB +qqA +L2A +I2B +L2B +I2A +sqA +sqB +AA +mnA +s2A +mnB +dqA +yn +LrA +p2A +s2B +tfB""".split()
+LAST = """BmA BmB tkB AB p2B LrB dqB f2A LmB ecg tB f2B tA ovB svB kA LmA ovA ckB svA ckA sgcB eoB kbB sgcA tkA kbA altB ceB eoA altA nlB ceA ynB +gqB nlA ynA +sn +gqA""".split()
+FIRST = """m7 m2 sn gpA m5 gqB gqA cB aA gpB spc txA aB LqB LqA cA txB IpA cqA sgA sgB pmA cvB cvA IpB fA cqB pmB cwA fB ofA qf m1 bA bc x1A cwB bB ofB x1B tfB rrA qqA qqB L2B SA rrB I2B L2A m6 sqA mnA m3 SB s2A AB I2A s2B dqA sqB BrB BrA tfA m4 BmA LrA ld p2B AA p2A dqB mnB f2B f2A g2""".split()
+ORDER = """tA ecg LmA +bc ovA ocB owB LrB svA ogB x2A ckA BmB sgcA eoA kbA tB LmB ovB svB altA ceA ckB x2B nlA +gqA sgcB kB +gpA eoB hd +aA +LqA +IpA +cA kbB +sgA altB ceB +txA +cqA +cB +pmA nlB +gqB +fA +cqB +cvB +aB +LqB +yn +gpB +IpB +cvA +sn +sgB +th +cwA +pmB +ofA +fB +x1A +cwB +bB +rrA +txB +ofB +sh +tfA +g2 +bA +rrB +SA +x1B +qqB +qqA +BrA +SB +I2A +L2A +I2B +L2B +s2A +AA +BrB +sqB +tfB +s2B +sqA +mnA +p2A +LrA +dqA +BmA +AB +dqB +mnB +f2A +p2B +f2B +hg""".split()
+LAST = """BmB ecg kB LrB tB tA LmB ovB LmA ovA svB kA svA ckB sgcB kbB tkA ckA tkB altB eoB ceB sgcA kbA eoA nlB +gqB +gpB altA ceA nlA ynB ynA +sn +gqA +gpA""".split()
+ONV = ["gqA", "gqB", "qqB", "kbA", "kbB"]
+FIRST = """i2 c2 c6 bc i1 c7 aB m1 n0 qf cA c1 c4 c5 gqB gqA spc aA cB LqA cvA LqB gpB gpA IpB sgA c3 cqA c8 IpA pmA m7 cqB sn sgB pmB fA m6 cwA cvB bA fB cwB txB ofA x1A ofB m2 m3 txA x1B rrB m8 rrA bB I2B BrB SB tfA qqB tfB L2B qqA sqB SA I2A AA mnB s2B L2A sqA dqB mnA BrA BmB dqA AB s2A p2B p2A BmA LrB m4 f2B f2A g2 ocB LrA LmA ovA tA m5 ld svA owB ecg""".split()
+ORDER = """+bc LmB ogB ovB tB ckA svB sgcA ckB hd kbA x2A eoA altA x2B +cA sgcB ceA kbB altB eoB ceB nlA +gqA nlB +gpA +aA +gpB +gqB +cqA +yn +LqA +IpA +txA +cvB +cvA +aB +cB +LqB +IpB +sgA +pmA +sgB +fA +cqB +th +txB +pmB +fB +sn +rrA +rrB +cwA +bB +cwB +ofA +x1A +I2A +SA +ofB +x1B +BrB +qqA +tfA +BrA +I2B +bA +qqB +tfB +L2B +L2A +SB +AA +sqA +AB +s2B +s2A +mnA +sqB +mnB +dqA +p2B +ocB +LrB +BmA +sh +p2A +BmB +LrA +LmA +dqB +f2A +f2B +hg +ovA +tA +g2 +owB +svA +ecg""".split()
+LAST = """LmB tB kB ovB svB ckA tkB sgcA kbA eoA kA ckB tkA sgcB altA kbB eoB ceA nlA ynA altB +gqA +gpA ceB nlB ynB +sn +gpB +gqB""".split()
 
 
 def emit(g, T, ops, final):
@@ -127,12 +150,12 @@ def rank_program(g, core, T, topo):
         op("X", None, [], keys, done=(sem, count))
         final.append((sem, count))
 
-    def hs(h): return slice(h * H, (h + 1) * H)
+    def hs(h, a=0): return slice(a + 16 * CUT[h], a + 16 * CUT[h + 1])
     def lst(buf, k, a=0, b=C): return buf[:, k * LS + a:k * LS + b]
     def nlst(k, a=0, b=C): return T.NL[:, k * C + a:k * C + b]
     def bank(i): return T["b%d" % i]
-    def bh(i): return bank(i)[:, 0:H]
-    def bl(i, n=C, a=0): return bank(i)[:, H + a:H + a + n]
+    def bh(i): return bank(i)[:, 0:16 * (CUT[i % 2 + 1] - CUT[i % 2])]
+    def bl(i, n): return bank(i)[:, LB:LB + n]
 
     eq, mul, add, sub = ALU.is_equal, ALU.mult, ALU.add, ALU.subtract
     Sign, Relu, Ident, Tanh = ACT.Sign, ACT.Relu, ACT.Identity, ACT.Tanh
@@ -157,12 +180,24 @@ def rank_program(g, core, T, topo):
     def mm(key, out, m, rhs, start, stop, rd):
         op("P", lambda: PE.matmul(out, m, rhs, start, stop), rd + ([] if start else [key]), [key, (key[0], "group")])
 
-    def conv(key, out, wt, src, a, n, start, stop, rd):
+    def turn(key, wt, n, src, lanes, rd):
+        rows = (lanes.stop - lanes.start) // 16
         for i in range(16):
-            mm(key, out, T[wt][:, 15 - i:143 - i], T[src][:, a + i:a + n:16], start and i == 0, stop and i == 15, rd + [wt])
+            mm(key, bank(key[0])[0:rows, i:16 * n:16], T[src][:, lanes.start + i:lanes.stop:16], wt, True, True, rd)
+
+    def conv(key, wt, src, lanes, start, stop, rd):
+        for i in range(16):
+            mm(key, bl(key[0], (lanes.stop - lanes.start) // 16), T[wt][:, 15 - i:143 - i], T[src][:, lanes.start + i:lanes.stop:16],
+               start and i == 0, stop and i == 15, rd + [wt])
+
+    def fetch(name, key, at, rows, slot):
+        scale_to(name, T.TT[0:rows, 128 * slot:128 * (slot + 1)], bank(key[0])[0:rows, at:at + 128], 1.0, [key], ["tt%d" % slot])
+
+    def back(key, rows, slot, wt, start, stop):
+        mm(key, bl(key[0], rows), T.TT[0:rows, 128 * slot:128 * (slot + 1)], T[wt][0:rows, 0:rows], start, stop, ["tt%d" % slot, wt])
 
     def uni(b, sel, buf, k, h, stop):
-        mm((b, "h"), bh(b), T[sel][0:8, :], T[buf][0:8, k * R + h * H:k * R + (h + 1) * H], True, stop, [sel, buf + ("1" if k else "0")])
+        mm((b, "h"), bh(b), T[sel][0:8, :], T[buf][0:8, hs(h, k * R)], True, stop, [sel, buf + ("1" if k else "0")])
 
     def load(e, name, out, src, key, after=()):
         q = g.sync if e == "Y" else g.scalar
@@ -175,77 +210,106 @@ def rank_program(g, core, T, topo):
     load("Y", "ua", T.UC[0:8, 0:R], T.ua[:, 0:R], "UC0")
     load("Y", "spot", T.spi[:], T.spot[:], "spi")
     load("Y", "ue", T.UD[0:8, R:], T.ud[:, R:], "UD1", ["P"])
-    load("Y", "nx", T.E[:], T.nx[:], "E")
 
     def spread(t):
         for x in range(16):
             op("Y", lambda x=x: g.sync.dma_start(T.UB[x:128:16, 2 * t * R:2 * (t + 1) * R], T.ua[:, (3 * t + 1) * R:3 * (t + 1) * R]),
-               ["NL%dA" % t], ["ub%d" % t] if x == 15 else [], done=("ub%d" % t, 256))
+               ["go%d" % (t - 1) if t else "P"], ["ub%d" % t] if x == 15 else [], done=("ub%d" % t, 256))
         final.append(("ub%d" % t, 256))
-        if t == 0:
-            load("Y", "ub", T.UC[0:8, 3 * R:], T.ua[:, 3 * R:], "UC1")
-            load("Y", "vf", T.F[:], T.vf[:], "F")
+
+    def rest():
+        load("Y", "nx", T.E[:], T.nx[:], "E", [LDKEY])
+        load("Y", "ub", T.UC[0:8, 3 * R:], T.ua[:, 3 * R:], "UC1")
+        load("Y", "vf", T.F[:], T.vf[:], "F")
 
     def iota(out, pat, cm, key):
         op("G", lambda: g.iota(out, pat, 0, cm, allow_small_or_imprecise_dtypes=True), [], [key])
-    op("G", lambda: g.iota(T.pi[:, 0:1], [[0, 1]], 0, 1), [], ["pi0"])
-    iota(T.gm[:], [[16, 8], [0, 16]], 0, "gm")
-    iota(T.um[:], [[1, 128]], -1, "um")
-    iota(T.ji[:], [[1, 144]], 0, "ji")
     def col(k): return T.col[:, k:k + 1]
-    PC, XC, G16, G15, R15, OM, G31, P16, X8 = range(9)
-    def scaled(items):
+    G16, XC, R2, OM, G32, P16 = range(6)
+    op("G", lambda: g.iota(T.pi[:, 0:1], [[0, 1]], 0, 1), [], ["pi0"])
+    iota(T.um[:], [[1, 128]], -1, "um")
+    iota(T.gm[:], [[16, 8], [0, 16]], 0, "gm")
+    iota(T.col[0:8, P16:P16 + 1], [[0, 1]], 16, "p16")
+    def numbers():
+        op("G", lambda: g.iota(T.ji[:], [[1, 144]], -15, 0, allow_small_or_imprecise_dtypes=True), [], ["ji"])
+    def numbers2():
+        op("G", lambda: g.iota(T.ti[:], [[1, 32]], 0, -1), [], ["ti"])
+        op("G", lambda: g.iota(T.tj[:], [[1, 128]], 0, -1), [], ["tj"])
+    def scaled(*items):
         for name, src, scale in items:
-            act(T[name][:], T[src][:], Ident, [src], [name], scale=scale)
-    ts(T.pi[:, 1:2], T.pi[:, 0:1], 15, None, ALU.bitwise_and, None, ["pi0"], ["pi1"])
-    cp(col(PC), T.pi[:, 0:1], ["pi0"], ["pc"])
-    cp(col(XC), T.pi[:, 1:2], ["pi1"], ["xc"])
-    ts(col(P16), col(PC), 16.0, None, mul, None, ["pc"], ["p16"])
-    tt(col(G16), col(PC), col(XC), sub, ["pc", "xc"], ["g16"])
-    ts(col(R15), col(XC), 15.0, None, eq, None, ["xc"], ["r15"])
-    ts(T.sN[0:8, :], T.gm[0:8, :], T.col[0:8, P16:P16 + 1], -1.0, eq, mul, ["gm", "p16"], ["sN"])
-    ts(T.blk[:], T.gm[:], col(G16), None, eq, None, ["gm", "g16"], ["blk"])
-    ts(col(G15), col(G16), 15.0, None, add, None, ["g16"], ["g15"])
-    ts(T.t0[:], T.um[:], 0.0, -0.5, ALU.is_ge, add, ["um"], ["t0"])
+            act(T[name][:], T[src][:, 0:T[name].shape[1]], Ident, [src], [name], scale=scale)
+    def summed(b, names):
+        for j, name in enumerate(names):
+            mm((b, "h"), bank(b)[:, 0:128], T.mI[:], T[name][:], j == 0, j == len(names) - 1, ["mI", name])
+    ts(T.pi[:, 1:2], T.pi[:, 0:1], 112, None, ALU.bitwise_and, None, ["pi0"], ["pi1"])
+    ts(T.pi[:, 2:3], T.pi[:, 0:1], 15, None, ALU.bitwise_and, None, ["pi0"], ["pi2"])
+    cp(T.col[:, G16:XC + 1], T.pi[:, 1:3], ["pi1", "pi2"], ["g16"])
     ts(T.mI[:], T.um[:], 0.0, None, eq, None, ["um"], ["mI"])
-    ts(T.t1[:], T.um[:], 1.0, -1.0, eq, mul, ["um"], ["t1"])
-    ts(T.t2[:], T.um[:], -15.0, -2.0, eq, add, ["um"], ["t2"])
-    act(T.sC[0:8, :], T.sN[0:8, :], Ident, ["sN"], ["sC"], scale=UNIT / 128)
-    scaled((("mP", "mI", UNIT),))
-    tt(T.t0[:], T.t0[:], T.blk[:], mul, ["t0", "blk"], ["t0"])
-    tt(T.t1[:], T.t1[:], T.mI[:], add, ["t1", "mI"], ["t1"])
-    ts(T.t2[:], T.t2[:], col(R15), None, mul, None, ["t2", "r15"], ["t2"])
-    ts(T.mN[:], T.t0[:], 0.0, -UNIT, ALU.is_gt, mul, ["t0"], ["mN"])
-    tt(T.t1[:], T.t1[:], T.t2[:], add, ["t1", "t2"], ["t1"])
-    ts(T.wW[:], T.ji[:], col(G15), float(W), eq, mul, ["ji", "g15"], ["wW"])
-    tt(T.t3[:], T.t1[:], T.blk[:], mul, ["t1", "blk"], ["t3"])
-    scaled((("mO1", "t3", 256.0),))
-    cp(T.hI[:], T.mI[:], ["mI"], ["hI"])
-    cp(nlst(0), T.n0i[:], ["n0i"], ["NL0A", "NL0B"])
 
-    def late():
-        scaled((("mB", "blk", 1.0 / 256), ("mL", "mN", -1.0 / UNIT), ("mR", "mI", 128.0), ("mO2", "t3", 2.0 ** 23), ("fB", "blk", -1.0),
-                ("mW", "mN", -128.0 / UNIT), ("fL", "mN", 128.0 / UNIT), ("mF", "t0", 2.0 ** 26), ("wX", "wW", 16.0 / W)))
-        ts(col(X8), col(XC), -1.0, -8.0, mul, add, ["xc"], ["x8"])
-        ts(col(OM), col(R15), 16.0, -1.0, mul, add, ["r15"], ["om"])
-        ts(col(G31), col(G16), 31.0, None, add, None, ["g16"], ["g31"])
-        act(T.t4[:], T.ji[:, 0:32], ACT.Abs, ["ji", "x8"], ["t4"], bias=col(X8))
-        ts(T.t5[:], T.blk[:], -2.0 ** 26, None, mul, None, ["blk"], ["t5"])
-        ts(T.mA[:], T.mI[:], 2.0 ** 27, None, mul, None, ["mI"], ["mA"])
-        ts(T.wK[:], T.ji[:], col(G15), col(OM), eq, mul, ["ji", "g15", "om"], ["wK"])
-        ts(T.w0[:], T.ji[:], col(G31), col(OM), eq, mul, ["ji", "g31", "om"], ["w0"])
-        ts(T.OH[:], T.t4[:], 8.0, None, eq, None, ["t4"], ["OH"])
-        cp(T.ti[:], T.um[:], ["um"], ["ti"])
-        tt(T.mA[:], T.mA[:], T.t5[:], add, ["mA", "t5"], ["mA"])
-        tt(T.wK[:], T.wK[:], T.w0[:], add, ["wK", "w0"], ["wK"])
-        ts(T.ti[:], T.ti[:], 159, None, ALU.bitwise_and, None, ["ti"], ["ti"])
-        ts(T.t1[:], T.ti[:], 0.0, None, eq, None, ["ti"], ["t1"])
-        ts(T.t2[:], T.ti[:], 16.0, -1.0, eq, mul, ["ti"], ["t2"])
+    def differences():
+        ts(col(R2), col(XC), 15.0, -2.0, eq, mul, ["g16"], ["r2"])
+        ts(T.t1[:], T.um[:], 1.0, -1.0, eq, mul, ["um"], ["t1"])
+        ts(T.t2[:], T.um[:], -15.0, col(R2), eq, add, ["um", "r2"], ["t2"])
+        summed(4, ["mI", "t1", "t2"])
+
+    def blocks():
+        ts(T.t0[:], T.um[:], 0.0, -0.5, ALU.is_ge, add, ["um"], ["t0"])
+        ts(T.blk[:], T.gm[:], col(G16), None, eq, None, ["gm", "g16"], ["blk"])
+        ts(T.sN[0:8, :], T.gm[0:8, :], T.col[0:8, P16:P16 + 1], -1.0, eq, mul, ["gm", "p16"], ["sN"])
+        tt(T.t0[:], T.t0[:], T.blk[:], mul, ["t0", "blk"], ["t0"])
+        ts(T.mN[:], T.t0[:], 0.0, -UNIT, ALU.is_gt, mul, ["t0"], ["mN"])
+
+    def either():
+        scaled(("t4", "mI", 2.0 ** 27), ("t5", "blk", -2.0 ** 26))
+        summed(2, ["t4", "t5"])
+    def either2():
+        act(T.mA[:], bank(2)[:, 0:128], Ident, [(2, "h")], ["mA"])
+
+    def verdicts():
+        ts(col(OM), col(R2), -8.0, -1.0, mul, add, ["r2"], ["om"])
+        ts(col(G32), col(G16), 16.0, None, add, None, ["g16"], ["g32"])
+        if "cvk" not in TURN:
+            ts(T.wK[:], T.ji[:], col(G16), col(OM), eq, mul, ["ji", "g16", "om"], ["wK"])
+            ts(T.w0[:], T.ji[:], col(G32), col(OM), eq, mul, ["ji", "g32", "om"], ["w0"])
+            tt(T.wK[:], T.wK[:], T.w0[:], add, ["wK", "w0"], ["wK"])
+            return
+        ts(T.gK[:, 8:16], T.gB[:], col(OM), None, mul, None, ["gB", "om"], ["gK1"])
+        ts(T.gK[:, 16:24], T.gm[:, 0:128:16], col(G32), col(OM), eq, mul, ["gm", "g32", "om"], ["gK2"])
+        tt(T.gK[:, 0:8], T.gK[:, 8:16], T.gK[:, 16:24], add, ["gK1", "gK2"], ["gK"])
+
+    def onehot():
+        ts(T.ti[:], T.ti[:], 15, None, ALU.bitwise_and, None, ["ti"], ["ti"])
+        ts(T.OH[:], T.ti[:], 0.0, None, eq, None, ["ti"], ["OH"])
+
+    def alternating():
+        ts(T.tj[:], T.tj[:], 159, None, ALU.bitwise_and, None, ["tj"], ["tj"])
+        ts(T.t1[:], T.tj[:], 0.0, None, eq, None, ["tj"], ["t1"])
+        ts(T.t2[:], T.tj[:], 16.0, -1.0, eq, mul, ["tj"], ["t2"])
         tt(T.mT[:], T.t1[:], T.t2[:], add, ["t1", "t2"], ["mT"])
+
+    def places():
+        cp(T.sp1[:], T.spi[:], ["spi"], ["sp1"])
+        cp(T.sph[:], T.sp1[:], ["sp1"], ["sph"])
+
+    later = {
+        "n0": lambda: cp(nlst(0), T.n0i[:], ["n0i"], ["NL0A", "NL0B"]),
+        "m1": lambda: scaled(("mL", "mN", -256.0 / UNIT), ("mR", "mI", 128.0)),
+        "m2": either, "m5": verdicts, "m6": onehot, "spc": places,
+        "m3": lambda: scaled(("mO2", "t3", 2.0 ** 23), ("fB", "blk", -1.0), ("mW", "mN", -128.0 / UNIT)),
+        "m4": lambda: scaled(("fL", "mN", 128.0 / UNIT), ("mF", "t0", 2.0 ** 26), ("wX", "wW", 16.0 / W)),
+        "m7": alternating, "ld": rest, "m8": either2, "i1": numbers, "i2": numbers2, "c1": differences, "c2": blocks,
+        "c3": lambda: tt(T.t3[:], T.blk[:], bank(4)[:, 0:128], mul, ["blk", (4, "h")], ["t3"]),
+        "c4": lambda: cp(T.hI[:], T.mI[:], ["mI"], ["hI"]),
+        "c5": lambda: ts(T.wW[:], T.ji[:], col(G16), float(W), eq, mul, ["ji", "g16"], ["wW"]),
+        "c6": lambda: scaled(("mP", "mI", UNIT)), "c8": lambda: scaled(("mO1", "t3", 256.0)),
+        "c7": lambda: act(T.sC[0:8, :], T.sN[0:8, :], Ident, ["sN"], ["sC"], scale=UNIT / 128),
+        "qf": lambda: scale_to("qf", T.Q[:, 0:W], T.Q0[:], 1.0 / UNIT, ["Q0"], ["Q"]),
+    }
 
     def share(src, dst, part, parts):
         es = topo.engines(src, dst)
         if parts > 1: es = [e for e in es if all(e in topo.engines(src, c) for c in T.cores if c != src)]
+        if FEW: es = es[::len(es) // min(len(topo.engines(src, c)) for c in T.cores if c != src)]
         return es[part * len(es) // parts:(part + 1) * len(es) // parts]
 
     def send(items, rd):
@@ -261,13 +325,14 @@ def rank_program(g, core, T, topo):
         op("G", call, rd, [], done=("sent", 0))
 
     def send_n(t):
-        items = [(nxt, lst(T.NI, t), [nlst(t)], "an%d" % t)]
-        if t in (2, 3): items.append((prv if t == 2 else opp, lst(T.HI, t - 2), [nlst(t)], "ah%d" % t))
-        send(items, ["NL%dA" % t, "NL%dB" % t])
-        arrives("an%d" % t, len(share(prv, core, 0, len(items))), ["NI%d" % t])
-        if t in (2, 3): arrives("ah%d" % t, len(share(nxt if t == 2 else opp, core, 1, 2)), ["HI%d" % (t - 2)])
+        send([(nxt, lst(T.NI, t), [nlst(t)], "an%d" % t)], ["NL%dA" % t, "NL%dB" % t])
+        arrives("an%d" % t, ne, ["NI%d" % t])
 
-    ne = len(topo.engines(prv, core))
+    def send_h(t):
+        send([(prv if t == 2 else opp, lst(T.HI, t - 2), [nlst(t)], "ah%d" % t)], ["NL%dA" % t, "NL%dB" % t])
+        arrives("ah%d" % t, len(share(nxt if t == 2 else opp, core, 0, 1)), ["HI%d" % (t - 2)])
+
+    ne = len(share(prv, core, 0, 1))
     X, Y, Z, U = (0, 1), (2, 3), (4, 5), (6, 7)
 
     def steps(t):
@@ -280,13 +345,12 @@ def rank_program(g, core, T, topo):
             nl = "NL%d" % t + k
             sl, x, y, z, u = hs(h), X[h], Y[h], Z[h], U[h]
             xh, yh, zh, uh, xl, yl, ul = (x, "h"), (y, "h"), (z, "h"), (u, "h"), (x, "l"), (y, "l"), (u, "l")
-            tl = slice(t * R + h * H, t * R + (h + 1) * H)
+            tl, c0, c1 = hs(h, t * R), CUT[h], CUT[h + 1]
+            n, ls = c1 - c0, slice(c0, c1)
             qs, ps, fs, rs, mn = T.q1[:, tl], T.p1[:, tl], T.fo1[:, tl], T.rr[:, sl], T.mn[:, sl]
             kq, kp, kf, kd, ki, kr, km = ["%s%d%s" % (s, t, k) for s in ("q1", "p1", "fo1", "di", "fi")] + ["rr" + k, "mn" + k]
-            own, inc = nlst(t, 18 * h, 18 * h + 18), lst(T.NI, t, 18 * h, 18 * h + 18)
-            ls = slice(18 * h, 18 * h + 18)
-            of1 = T.OF1[:, ls]
-            ub = [T.UB[:, (2 * t + j) * R + h * H:(2 * t + j) * R + (h + 1) * H] for j in (0, 1)]
+            own, inc = nlst(t, c0, c1), lst(T.NI, t, c0, c1)
+            ub = [T.UB[:, hs(h, (2 * t + j) * R)] for j in (0, 1)]
             def lanes(name, land, srcs):
                 ks = "AB" if name in WHOLE else k
                 if ks[-1] != k: return
@@ -294,34 +358,41 @@ def rank_program(g, core, T, topo):
                 send([(nxt, T[land][:, a], [T[s][:, a] for s in srcs], "%s%s%d" % (name, k, t))],
                      ["%s%d%s" % (s, t, j) for s in srcs for j in ks])
                 arrives("%s%s%d" % (name, k, t), ne, ["%si%d%s" % (name, t, j) for j in ks])
-            def tx(): lanes("d", "DI", ["p1", "q1"])
-            def tf(): lanes("f", "FI", ["fo1"])
             def gq():
                 if t == 0: scale_to("gq" + k, qs, T.Q0[:].indirect(own), -1.0 / UNIT, ["Q0", nl], [kq])
                 else: scale_to("gq" + k, qs, T.Q[:, 0:W].indirect(own), -1.0, ["Q", nl], [kq])
             def rr():
                 if "rr" + k in ONV: ts(rs, T.DI[:, tl], 0.0, 256.0 * UNIT, ALU.max, mul, [kd], [kr])
                 else: act(rs, T.DI[:, tl], Relu, [kd], [kr], scale=256.0 * UNIT)
+            def offsets(key, slot):
+                mm(key, bl(key[0], n), T.hI[:], T.sph[:, t * C + c0:t * C + c1], True, False, ["hI", "sph"])
+                back(key, n, slot, "wI", False, True)
+            def x2(a, b):
+                op("S", lambda: S.activation(T.Q[:].indirect(T.OF2[:, a:b]), T.p2[:, 16 * a:16 * b], Tanh), ["of2" + k, "p2"], ["Q"])
             d = {
                 "a": lambda: uni(x, "sN", "UD", 2 * t, h, False),
                 "c": lambda: uni(y, "sC", "UC", 3 * t, h, True),
-                "p": lambda: mm(ul, bl(u, 18), T.hI[:], T.sph[:, t * C + 18 * h:t * C + 18 * h + 18], True, False, ["hI", "sph"]),
                 "gq": gq,
                 "gp": lambda: scale_to("gp" + k, ps, T.P[:].indirect(own), 1.0 / UNIT, ["P", nl], [kp]),
-                "tx": tx, "tf": tf,
+                "tx": lambda: lanes("d", "DI", ["p1", "q1"]),
                 "Lq": lambda: mm(xh, bh(x), T.mN[:], qs, False, True, ["mN", kq]),
                 "Ip": lambda: mm(zh, bh(z), T.mP[:], ps, True, False, ["mP", kp]),
                 "sg": lambda: act(T.s1[:, sl], bh(x), Sign, [xh], ["s1" + k], bias=-0.5),
                 "cq": lambda: tt(T.cq[:, sl], qs, bh(y), mul, [kq, yh], ["cq" + k]),
                 "pm": lambda: mm(zh, bh(z), T.mO1[:], T.s1[:, sl], False, True, ["mO1", "s1" + k]),
                 "f": lambda: tt(fs, T.cq[:, sl], bh(z), ALU.is_lt, ["cq" + k, zh], [kf]),
-                "cv": lambda: conv(ul, bl(u, 18), "wW", "fo1", t * R + h * H, H, False, True, [kf]),
-                "of": lambda: cp(of1, bl(u, 18), [ul], ["of1" + k]),
-                "x1": lambda: cp(T.Q[:].indirect(of1), ps, ["of1" + k, kp], ["Q"]),
+                "tf": lambda: lanes("f", "FI", ["fo1"]),
+                "cv": lambda: turn(uh, T.gB[:], 8, "fo1", tl, [kf, "gB"]),
+                "ev": lambda: fetch("ev" + k, uh, 0, n, h),
+                "cw": lambda: offsets(ul, h),
+                "of": lambda: cp(T.OF1[:, ls], bl(u, n), [ul], ["of1" + k]),
+                "x1": lambda: cp(T.Q[:].indirect(T.OF1[:, ls]), ps, ["of1" + k, kp], ["Q"]),
                 "rr": rr,
                 "b": lambda: uni(z, "sN", "UD", 2 * t + 1, h, False),
-                "S": lambda: mm(yh, bh(y), T.mB[:], rs, True, True, ["mB", kr]),
-                "qq": lambda: scale_to("qq" + k, T.q2[:, sl], T.Q[:, 0:W].indirect(inc), UNIT, ["Q", ni], ["q2" + k]),
+                "S": lambda: mm(yh, bh(y), T.blk[:], rs, True, True, ["blk", kr]),
+                "Br": lambda: mm(uh, bh(u), T.blk[:], rs, True, False, ["blk", kr]),
+                "qq": lambda: scale_to("qq" + k, T.q2[:, sl], T.Q[:, 0:W].indirect(inc), UNIT / 256, ["Q", ni],
+                                       ["q2" + k] + (["go%d" % t] if h == 0 else [])),
                 "sq": lambda: tt(bh(y), T.q2[:, sl], bh(y), mul, ["q2" + k, yh], [yh]),
                 "L2": lambda: mm(zh, bh(z), T.mL[:], T.q2[:, sl], False, True, ["mL", "q2" + k]),
                 "s2": lambda: act(T.s2[:, sl], bh(z), Sign, [zh], ["s2" + k], bias=-0.5),
@@ -331,50 +402,94 @@ def rank_program(g, core, T, topo):
                 "dq": lambda: tt(T.dq[:, sl], ub[0], bh(y), mul, ["ub%d" % t, yh], ["dq" + k]),
                 "f2": lambda: tt(T.fo2[:, sl], T.dq[:, sl], bh(x), ALU.is_lt, ["dq" + k, xh], ["fo2" + k]),
                 "mn": lambda: tt(mn, rs, bh(y), ALU.min, [kr, yh], [km]),
-                "Br": lambda: mm(uh, bh(u), T.blk[:], rs, True, False, ["blk", kr]),
                 "Bm": lambda: mm(uh, bh(u), T.fB[:], mn, False, True, ["fB", km]),
                 "Lr": lambda: mm(zh, bh(z), T.mW[:], rs, True, False, ["mW", kr]),
                 "Lm": lambda: mm(zh, bh(z), T.fL[:], mn, False, False, ["fL", km]),
                 "ov": lambda: mm(zh, bh(z), T.mF[:], T.fo2[:, sl], False, True, ["mF", "fo2" + k]),
                 "t": lambda: tt(T.th[:, sl], ub[1], bh(u), mul, ["ub%d" % t, uh], ["th" + k]),
                 "sv": lambda: tt(T.sv[:, sl], T.th[:, sl], bh(z), ALU.is_lt, ["th" + k, zh], ["sv" + k]),
-                "cvk": lambda: conv(yl, bl(y, 18), "wK", "sv", h * H, H, True, True, ["sv" + k]),
-                "sgc": lambda: cp(T.SG[:, ls], bl(y, 18), [yl], ["sg" + k]),
-                "kb": lambda: act(T.KB[:, ls], bl(y, 18), Ident, [yl], ["kb" + k]),
-                "alt": lambda: mm(xl, bl(x, 18), T.mT[:], T.KB[:, ls], True, False, ["mT", "kb" + k]),
+                "cvk": lambda: turn(yh, T.gK[:, 0:16], 16, "sv", sl, ["sv" + k, "gK"]),
+                "ek": lambda: fetch("ek" + k, yh, 0, n, 2 + h),
+                "ck": lambda: back(yl, n, 2 + h, "mI", True, True),
+                "sgc": lambda: cp(T.SG[:, ls], bl(y, n), [yl], ["sg" + k]),
+                "kb": lambda: fetch("kb" + k, yh, 128, n, 4 + h),
+                "alt": lambda: back(ul, n, 4 + h, "mI", True, False),
                 "eo": lambda: tt(T.eo[:, sl], T.OH[:].indirect(T.SG[:, ls]), T.ec[:, sl], mul, ["OH", "sg" + k, "ec"], ["eo" + k]),
-                "cve": lambda: conv(xl, bl(x, 18), "wX", "eo", h * H, H, False, True, ["eo" + k]),
-                "nl": lambda: cp(nlst(t + 1, 18 * h, 18 * h + 18), bl(x, 18), [xl], ["NL%d" % (t + 1) + k]),
+                "cve": lambda: turn(zh, T.gB[:], 8, "eo", sl, ["eo" + k, "gB"]),
+                "ee": lambda: fetch("ee" + k, zh, 0, n, 6 + h),
+                "ce": lambda: back(ul, n, 6 + h, "xI", False, True),
+                "nl": lambda: cp(nlst(t + 1, c0, c1), bl(u, n), [ul], ["NL%d" % (t + 1) + k]),
             }
             if last:
-                d["yn"] = lambda: act(T.YN[:, t * C + 18 * h:t * C + 18 * h + 18], bl(x, 18), Ident, [xl], ["yn" + k])
+                d["yn"] = lambda: act(T.YN[:, t * C + c0:t * C + c1], bl(u, n), Ident, [ul], ["yn" + k])
                 d["k"] = lambda: tt(T.hx[:, sl], T.F[:].indirect(inc), T.hh[:, sl], add, ["F", ni, "hh" + k], ["hx" + k])
                 d["tk"] = lambda: act(T.hh[:, sl], T.hx[:, sl], Tanh, ["hx" + k], ["hh" + k])
+            else:
+                mid = c0 + n // 4 * 2
+                d["oc"] = lambda: turn(xh, T.gB[:], 8, "fo2", sl, ["fo2" + k, "gB"])
+                d["oe"] = lambda: fetch("oe" + k, xh, 0, n, 8 + h)
+                d["ow"] = lambda: offsets(xl, 8 + h)
+                d["og"] = lambda: cp(T.OF2[:, ls], bl(x, n), [xl], ["of2" + k])
+                d["x2"] = lambda: x2(c0, mid)
+                d["y2"] = lambda: x2(mid, c1)
+            def place(key):
+                mm(key, bl(key[0], n), T.hI[:], T.sph[:, t * C + c0:t * C + c1], True, False, ["hI", "sph"])
+            if "cv" not in TURN:
+                d["cv"] = lambda: place(ul)
+                d["cw"] = lambda: conv(ul, "wW", "fo1", tl, False, True, [kf])
+                del d["ev"]
+            if "oc" not in TURN and not last:
+                d["oc"] = lambda: place(xl)
+                d["ow"] = lambda: conv(xl, "wW", "fo2", sl, False, True, ["fo2" + k])
+                del d["oe"]
+            if "cve" not in TURN:
+                d["ce"] = lambda: conv(ul, "wX", "eo", sl, False, True, ["eo" + k])
+                del d["cve"], d["ee"]
+            if "cvk" not in TURN:
+                d["ck"] = lambda: conv(yl, "wK", "sv", sl, True, True, ["sv" + k])
+                d["kb"] = lambda: scale_to("kb" + k, T.KB[:, ls], bl(y, n), 1.0, [yl], ["kb" + k])
+                d["alt"] = lambda: mm(ul, bl(u, n), T.mT[:], T.KB[:, ls], True, False, ["mT", "kb" + k])
+                del d["cvk"], d["ek"]
+            if WIDE and not last:
+                if h == 0: del d["oc"], d["ow"], d["og"]
+                else:
+                    d["oc"] = lambda: mm(xl, bl(x, C), T.hI[:], T.sph[:, t * C:(t + 1) * C], True, False, ["hI", "sph"])
+                    d["ow"] = lambda: conv(xl, "wW", "fo2", slice(0, R), False, True, ["fo2A", "fo2B"])
+                    d["og"] = lambda: cp(T.OF2[:], bl(x, C), [xl], ["of2A", "of2B"])
+            if "k" in BOTH:
+                if h == 0: del d["ck"], d["sgc"], d["kb"]
+                else:
+                    d["ck"] = lambda: conv(yl, "wK", "sv", slice(0, R), True, True, ["svA", "svB"])
+                    d["sgc"] = lambda: cp(T.SG[:], bl(y, C), [yl], ["sgA", "sgB"])
+                    d["kb"] = lambda: scale_to("kb" + k, T.KB[:], bl(y, C), 1.0, [yl], ["kbA", "kbB"])
+            if "e" in BOTH:
+                if h == 0:
+                    del d["alt"], d["ce"], d["nl"]
+                    if last: del d["yn"]
+                else:
+                    d["alt"] = lambda: mm(ul, bl(u, C), T.mT[:], T.KB[:], True, False, ["mT", "kbA", "kbB"])
+                    d["ce"] = lambda: conv(ul, "wX", "eo", slice(0, R), False, True, ["eoA", "eoB"])
+                    d["nl"] = lambda: cp(nlst(t + 1), bl(u, C), [ul], ["NL%dA" % (t + 1), "NL%dB" % (t + 1)])
+                    if last: d["yn"] = lambda: act(T.YN[:, t * C:(t + 1) * C], bl(u, C), Ident, [ul], ["ynA", "ynB"])
+            if not last and k not in SPLIT:
+                d["x2"] = lambda: x2(c0, c1)
+                del d["y2"]
             for name in d:
                 st[name + k] = d[name]
         half(0)
         half(1)
 
-        ol, oa = (Y[1], "o"), bl(Y[1], C, 32)
-        def x2(j):
-            a, b = X2CUT[j], X2CUT[j + 1]
-            if b > a: op("S", lambda: S.activation(T.Q[:].indirect(T.OF2[:, a:b]), T.p2[:, 16 * a:16 * b], Tanh), ["of2", "p2"], ["Q"])
         hh, hx = ["hhA", "hhB"], ["hxA", "hxB"]
         st.update({
             "sn": lambda: send_n(t), "bc": lambda: spread(t),
             "ecg": lambda: scale_to("ecg", T.ec[:], T.E[:].indirect(lst(T.NI, t)), 1.0, ["E", ni], ["ec"]),
         })
         if not last:
-            st.update({
-                "g2": lambda: scale_to("g2", T.p2[:], T.P[:].indirect(lst(T.NI, t)), 1.0 / UNIT, ["P", ni], ["p2"]),
-                "o2p": lambda: mm(ol, oa, T.hI[:], T.sph[:, t * C:(t + 1) * C], True, False, ["hI", "sph"]),
-                "o2c": lambda: conv(ol, oa, "wW", "fo2", 0, R, False, True, ["fo2A", "fo2B"]),
-                "of2": lambda: cp(T.OF2[:], oa, [ol], ["of2"]),
-                "x2a": lambda: x2(0), "x2b": lambda: x2(1), "x2c": lambda: x2(2),
-            })
+            st["g2"] = lambda: scale_to("g2", T.p2[:], T.P[:].indirect(lst(T.NI, t)), 1.0 / UNIT, ["P", ni], ["p2"])
         if t == 1:
             st["th"] = lambda: act(T.hh[:], T.F[:].indirect(nlst(1)), Tanh, ["F", "NL1A", "NL1B"], hh)
         if t in (2, 3):
+            st["sh"] = lambda: send_h(t)
             st["hg"] = lambda: act(T.hx[:], T.F[:].indirect(lst(T.HI, t - 2)), Ident, ["F", "HI%d" % (t - 2)], hx)
             st["hd"] = lambda: op("G", lambda: g.dma_start(T.hh[:], T.hx[:], accum_op=add), hx + hh, hh, done=("hd%d" % t, 16))
         if t in (3, 4):
@@ -385,28 +500,22 @@ def rank_program(g, core, T, topo):
 
     def out_h(k, a, b):
         sl = slice(16 * a, 16 * b)
-        tt(T.hx[:, sl], T.F[:].indirect(nlst(TK, a, b)), T.hh[:, sl], add, ["F", "NL%d" % TK + k, "hh" + k], ["hz%d" % a, "hx" + k])
+        tt(T.hx[:, sl], T.F[:].indirect(nlst(TK, a, b)), T.hh[:, sl], add, ["F", "NL%d" % TK + k, "hh" + k], ["hz%d" % a])
         act(T.ho[:, sl], T.hx[:, sl], Tanh, ["hz%d" % a], ["ho%d" % a])
         op("Y", lambda: g.sync.dma_start(T.yh[:, sl], T.ho[:, sl]), ["ho%d" % a], [], done=("stored", 16))
-
-    def out_b():
-        for a, b in zip(TAIL, TAIL[1:]): out_h("B", a, b)
 
     def out_n():
         op("S", lambda: g.scalar.dma_start(T.yn[:], T.YN[:]), ["yn", "ynA", "ynB"], [], done=("stored", 16))
 
-    def places():
-        cp(T.sp1[:], T.spi[:], ["spi"], ["sp1"])
-        cp(T.sph[:], T.sp1[:], ["sp1"], ["sph"])
-
-    every = [steps(t) for t in range(TK)] + [{"gqA": lambda: out_h("A", 0, 18), "gqB": out_b, "sn": out_n}]
-    every[0].update({"spc": places, "late": late,
-                     "qf": lambda: ts(T.Q[:, 0:W], T.Q0[:], 1.0 / UNIT, None, mul, None, ["Q0"], ["Q"])})
+    every = [steps(t) for t in range(TK)] + [{
+        "gqA": lambda: out_h("A", 0, TAIL[0]), "gpA": lambda: out_h("A", TAIL[0], CUT[1]),
+        "gqB": lambda: out_h("B", CUT[1], TAIL[1]), "gpB": lambda: out_h("B", TAIL[1], C), "sn": out_n}]
+    every[0].update(later)
     for t, names in [(0, FIRST)] + [(t, ORDER) for t in range(TK - 1)] + [(TK - 1, LAST)]:
         for name in names:
             u = t + 1 if name[0] == "+" else t
             now[0] = name.lstrip("+") + str(u)
             if name.lstrip("+") in every[u]: every[u][name.lstrip("+")]()
-    final.append(("stored", 16 * (len(TAIL) + 1)))
+    final.append(("stored", 16 * 5))
     final.append(("sent", sent[0]))
     emit(g, T, ops, final)

from concourse.bass import DstId, RemoteDMATransfer
from concourse.mybir import AluOpType as ALU, ActivationFunctionType as ACT

W, R, TK, C = 1280, 576, 5, 36
CUT = [0, 18, 36]
LB = 352
LS = 40
UNIT = 4096.0

SCRATCH = {
    "Q": ("sbuf", [128, 2 * W], "float32"), "Q0": ("sbuf", [128, W], "bfloat16"), "P": ("sbuf", [128, W], "bfloat16"),
    "E": ("sbuf", [128, W], "bfloat16"), "F": ("sbuf", [128, W], "bfloat16"),
    "UD": ("sbuf", [128, 2 * TK * R], "bfloat16"), "UC": ("sbuf", [128, 3 * TK * R], "bfloat16"),
    "UB": ("sbuf", [128, 2 * TK * R], "bfloat16"),
    "n0i": ("sbuf", [128, C], "int32"), "spi": ("sbuf", [128, TK * C], "int32"),
    "sp1": ("sbuf", [128, TK * C], "float32"), "sph": ("sbuf", [128, TK * C], "float16"),
    "NL": ("sbuf", [128, (TK + 1) * C], "uint16"), "NI": ("sbuf", [128, TK * LS], "uint16"),
    "HI": ("sbuf", [128, 2 * LS], "uint16"),
    "OF1": ("sbuf", [128, C], "uint16"), "OF2": ("sbuf", [128, C], "uint16"),
    "SG": ("sbuf", [128, C], "uint16"), "YN": ("sbuf", [128, TK * C], "float32"),
    "pi": ("sbuf", [128, 4], "int32"), "col": ("sbuf", [128, 16], "bfloat16"), "ti": ("sbuf", [128, 32], "int32"),
    "OH": ("sbuf", [128, 32], "bfloat16"), "hI": ("sbuf", [128, 128], "float16"),
    "ji": ("sbuf", [128, 144], "bfloat16"), "wW": ("sbuf", [128, 144], "bfloat16"), "wX": ("sbuf", [128, 144], "bfloat16"),
    "wK": ("sbuf", [128, 144], "bfloat16"), "w0": ("sbuf", [128, 144], "bfloat16"), "KB": ("sbuf", [128, C], "bfloat16"),
    "mT": ("sbuf", [128, 128], "bfloat16"), "tj": ("sbuf", [128, 128], "int32"),
    "gB": ("sbuf", [128, 8], "bfloat16"), "gK": ("sbuf", [128, 24], "bfloat16"),
    "wI": ("sbuf", [128, C], "bfloat16"), "xI": ("sbuf", [128, C], "bfloat16"), "TT": ("sbuf", [128, 10 * 128], "bfloat16"),
}
for _n in ("p1", "q1", "fo1", "DI", "FI"):
    SCRATCH[_n] = ("sbuf", [128, TK * R], "bfloat16")
for _n in ("s1", "rr", "q2", "s2", "fo2", "sv", "ec", "eo"):
    SCRATCH[_n] = ("sbuf", [128, R], "bfloat16")
for _n in ("cq", "p2", "mn", "th", "dq", "hh", "hx", "ho"):
    SCRATCH[_n] = ("sbuf", [128, R], "float32")
for _n in ("mL", "mN", "mI", "mP", "mR", "mW", "mO1", "mO2", "mB", "mF", "mA", "sN", "sC",
           "um", "gm", "blk", "t0", "t1", "t2", "t3", "t4", "t5"):
    SCRATCH[_n] = ("sbuf", [128, 128], "bfloat16")
for _n in ("fL", "fB"):
    SCRATCH[_n] = ("sbuf", [128, 128], "float32")
for _i in range(8):
    SCRATCH["b%d" % _i] = ("psum", [128, 512], "float32")

LOADS = ["n0", "qd", "pt", "ud", "ue", "ua", "ub", "spot", "nx", "vf"]
SEMAPHORES = (["cV", "cS", "cP", "cG", "sent", "stored", "ah2", "ah3", "hd2", "hd3"] + ["ld_" + n for n in LOADS]
              + ["%s%d" % (k, t) for t in range(TK) for k in ("an", "dA", "dB", "fA", "fB", "ub")])

ONV = ["gpA", "gqB", "qqB"]
WHOLE = ""
TURN = []
WIDE = True
SPLIT = ""
BOTH = ""
LDKEY = "go0"
FEW = True
TAIL = [10, 28]
FIRST = """m1 m2 m3 m4 m5 m6 bc sn aA aB cA cB gpA gqA gqB LqA IpA gpB txA cqA sgA LqB IpB txB spc qf pmA cqB sgB fA pmB cvA evA cwA tfA fB tfB cvB evB cwB
ofA x1A rrA rrB th bA bB SA SB I2A I2B BrA BrB ofB g2 ecg x1B""".split()
ORDER = """qqA qqB AA AB L2A sqA mnA L2B s2A s2B BmA sqB mnB p2A LrA LmA dqA f2A p2B dqB f2B ovA tA svA ocA oeA owA ogA ocB oeB owB ogB LrB BmB hg hd kA
x2A cvkA ekA ckA tB LmB ovB svB sgcA kbA eoA y2A cvkB ekB ckB altA cveA eeA ceA kB tkA sgcB kbB eoB x2B y2B altB cveB eeB ceB nlA ynA tkB nlB ynB +bc
+sn +aA +aB +cA +cB +gpA +gqA +gqB +LqA +IpA +gpB +txA +cqA +sgA +LqB +IpB +txB +pmA +cqB +sgB +fA +pmB +cvA +evA +cwA +tfA +fB +tfB +cvB +evB
+cwB +ofA +x1A +rrA +rrB +th +yn +bA +bB +SA +SB +I2A +I2B +BrA +BrB +ofB +g2 +ecg +x1B""".split()
FIRST = """aA m6 gqA qf sn m5 gqB gpB gpA aB LqA cA IpA LqB sgA sgB cB pmA spc cqA IpB txA fA cvA m2 cqB evA pmB cwA fB m3 cvB txB evB m1 ofA x1A m4 cwB rrA bB ofB SA x1B bA""".split()
ORDER = """bc qqB tfA qqA L2A s2A rrB sqA mnA L2B BrA dqA tfB I2A LrA BmA s2B SB LmA AA hg p2A sqB I2B LrB mnB f2A tA BrB ovA svA BmB ecg ocA g2 cvkA oeA AB ekA dqB kbA tB p2B owA LmB ckA ogA f2B ocB x2A ovB oeB sgcA y2A eoA owB cveA svB altA +aA hd eeA ogB cvkB x2B ceA ekB y2B nlA +gqA +cA ckB +aB +gpA sgcB eoB cveB +cqA kbB eeB +LqA +sgA altB +IpA +txA ceB +cB +pmA nlB +gqB +gpB +fA +LqB +cqB +IpB +sn +sgB +txB +cvA +evA +pmB +fB +th +cwA +cvB +bA +bB +evB +ofA +cwB +x1A +rrA +ofB +x1B +SA""".split()
LAST = """BrA qqA qqB L2A bc tfA s2A tfB L2B sqA I2A mnA kB LrA kA LmA dqA s2B rrB SB sqB mnB BmA BrB LrB tkB yn AA dqB p2A I2B BmB f2A AB p2B tB ecg LmB f2B ovB tA ovA svB cvkB tkA svA ekB cvkA kbA ekA ckB ckA sgcB eoB kbB sgcA cveB eeB eoA altB ceB nlB cveA eeA altA ceA ynB ynA +sn +gqB nlA +gqA""".split()
ONV = ["gqA", "gqB", "qqB"]
CUT = [0, 20, 36]
FIRST = """bc m2 m1 m7 gqA m5 gqB aA aB cB cA LqA spc cqA gpA LqB gpB sgA sgB sn IpA cqB txA qf IpB pmA fA pmB fB cvB m4 cvA m3 cwA cwB txB rrA tfA ofA x1A ofB x1B qqA ld rrB bA SA bB m6 L2A qqB sqA L2B I2A mnA dqA SB s2A I2B AA LrA sqB dqB s2B BmA mnB p2A""".split()
ORDER = """tfB ecg g2 f2A AB hd p2B ocB LmA f2B ovA owB tA LrB svA ogB ckA BmB LmB ovB x2A sgcA kbA eoA tB svB x2B altA ceA nlA ckB +cA +aA +aB +bc +gqA sgcB eoB +gpA +LqA kbB +sgA altB ceB +cvA +IpA +cqA nlB +pmA +cvB +gqB +txA +cB +fA +LqB +sn +gpB +yn +cqB +IpB +sgB +cwA +th +rrA +hg +pmB +ofA +fB +x1A +cwB +txB +ofB +x1B +SA +qqA +bA +I2A +bB +rrB +L2A +kB +qqB +L2B +s2A +SB +sqA +I2B +tfA +mnA +AA +sqB +dqA +mnB +dqB +p2A +s2B +LrA +BmA""".split()
LAST = """tkB tA LrB tfB AB ecg p2B BmB LmB f2B ovB tB f2A svB LmA ovA ckB kA svA sgcB ckA eoB sgcA kbB tkA altB kbA eoA ceB altA ceA nlB +gqB nlA ynA ynB +sn +gqA""".split()
FIRST = """m2 m7 gpB gqA m5 gqB gpA spc cB aA aB LqA LqB sn IpB IpA cA sgA sgB txA qf pmA cvA pmB cvB cqB cqA txB fA cwA m3 m1 tfA fB ofA bA cwB tfB x1A bc ofB rrA x1B qqA rrB SA BrA I2A bB L2A s2A m4 m6 qqB sqA SB I2B BrB L2B mnA sqB AA mnB p2A LrA s2B dqA ld""".split()
ORDER = """hd BmA dqB f2A ecg AB p2B f2B LmA g2 ovA ocB owB LrB tA svA ogB x2A ckA BmB LmB sgcA eoA ovB kbA altA tB svB ceA nlA x2B +gpA +gqA ckB +aA +cA sgcB kbB +LqA +IpA +sgA +cvA altB eoB ceB +cqA nlB +pmA +cvB +cB +aB +txA +gqB +fA +cqB +LqB +gpB +sn +txB +IpB +bc +cwA +sgB +ofA +pmB +fB +th +x1A +cwB +rrA +hg +rrB +BrA +bA +SA +bB +ofB +tfA +BrB +x1B +kB +qqB +SB +qqA +L2A +I2B +L2B +I2A +sqA +sqB +AA +mnA +s2A +mnB +dqA +yn +LrA +p2A +s2B +tfB""".split()
LAST = """BmA BmB tkB AB p2B LrB dqB f2A LmB ecg tB f2B tA ovB svB kA LmA ovA ckB svA ckA sgcB eoB kbB sgcA tkA kbA altB ceB eoA altA nlB ceA ynB +gqB nlA ynA +sn +gqA""".split()
FIRST = """m7 m2 sn gpA m5 gqB gqA cB aA gpB spc txA aB LqB LqA cA txB IpA cqA sgA sgB pmA cvB cvA IpB fA cqB pmB cwA fB ofA qf m1 bA bc x1A cwB bB ofB x1B tfB rrA qqA qqB L2B SA rrB I2B L2A m6 sqA mnA m3 SB s2A AB I2A s2B dqA sqB BrB BrA tfA m4 BmA LrA ld p2B AA p2A dqB mnB f2B f2A g2""".split()
ORDER = """tA ecg LmA +bc ovA ocB owB LrB svA ogB x2A ckA BmB sgcA eoA kbA tB LmB ovB svB altA ceA ckB x2B nlA +gqA sgcB kB +gpA eoB hd +aA +LqA +IpA +cA kbB +sgA altB ceB +txA +cqA +cB +pmA nlB +gqB +fA +cqB +cvB +aB +LqB +yn +gpB +IpB +cvA +sn +sgB +th +cwA +pmB +ofA +fB +x1A +cwB +bB +rrA +txB +ofB +sh +tfA +g2 +bA +rrB +SA +x1B +qqB +qqA +BrA +SB +I2A +L2A +I2B +L2B +s2A +AA +BrB +sqB +tfB +s2B +sqA +mnA +p2A +LrA +dqA +BmA +AB +dqB +mnB +f2A +p2B +f2B +hg""".split()
LAST = """BmB ecg kB LrB tB tA LmB ovB LmA ovA svB kA svA ckB sgcB kbB tkA ckA tkB altB eoB ceB sgcA kbA eoA nlB +gqB +gpB altA ceA nlA ynB ynA +sn +gqA +gpA""".split()
ONV = ["gqA", "gqB", "qqB", "kbA", "kbB"]
FIRST = """i2 c2 c6 bc i1 c7 aB m1 n0 qf cA c1 c4 c5 gqB gqA spc aA cB LqA cvA LqB gpB gpA IpB sgA c3 cqA c8 IpA pmA m7 cqB sn sgB pmB fA m6 cwA cvB bA fB cwB txB ofA x1A ofB m2 m3 txA x1B rrB m8 rrA bB I2B BrB SB tfA qqB tfB L2B qqA sqB SA I2A AA mnB s2B L2A sqA dqB mnA BrA BmB dqA AB s2A p2B p2A BmA LrB m4 f2B f2A g2 ocB LrA LmA ovA tA m5 ld svA owB ecg""".split()
ORDER = """+bc LmB ogB ovB tB ckA svB sgcA ckB hd kbA x2A eoA altA x2B +cA sgcB ceA kbB altB eoB ceB nlA +gqA nlB +gpA +aA +gpB +gqB +cqA +yn +LqA +IpA +txA +cvB +cvA +aB +cB +LqB +IpB +sgA +pmA +sgB +fA +cqB +th +txB +pmB +fB +sn +rrA +rrB +cwA +bB +cwB +ofA +x1A +I2A +SA +ofB +x1B +BrB +qqA +tfA +BrA +I2B +bA +qqB +tfB +L2B +L2A +SB +AA +sqA +AB +s2B +s2A +mnA +sqB +mnB +dqA +p2B +ocB +LrB +BmA +sh +p2A +BmB +LrA +LmA +dqB +f2A +f2B +hg +ovA +tA +g2 +owB +svA +ecg""".split()
LAST = """LmB tB kB ovB svB ckA tkB sgcA kbA eoA kA ckB tkA sgcB altA kbB eoB ceA nlA ynA altB +gqA +gpA ceB nlB ynB +sn +gpB +gqB""".split()


def emit(g, T, ops, final):
    queue = {"V": g.vector, "S": g.scalar, "P": g.tensor, "G": g, "Y": g.sync}
    last_w, readers, last_b, deps = {}, {}, {}, []
    for i, (e, fn, rd, wr, bk, done, name) in enumerate(ops):
        d = set()
        for k in rd:
            d.add(last_w[k])
        for k in wr:
            d.update(readers.get(k, []) + ([last_w[k]] if k in last_w else []))
        for k in bk:
            if k in last_b and ops[last_b[k]][0] != e: d.add(last_b[k])
        d.discard(i)
        deps.append({j for j in d if not (e == "P" and ops[j][0] == "P")})
        for k in rd: readers.setdefault(k, []).append(i)
        for k in wr:
            last_w[k] = i
            readers[k] = []
        for k in bk: last_b[k] = i
    pos, cnt = [], {}
    for op in ops:
        cnt[op[0]] = cnt.get(op[0], 0) + 1
        pos.append(cnt[op[0]])
    know = {e: {} for e in list(queue) + ["X"]}
    clock, waits, needed = [], [], set()
    for i, (e, fn, rd, wr, bk, done, name) in enumerate(ops):
        w = []
        for j in sorted(deps[i], reverse=True):
            key = ops[j][5][0] if ops[j][5] is not None else ops[j][0]
            if know[e].get(key, 0) >= pos[j]: continue
            w.append(j)
            needed.add(j)
            for k, v in clock[j].items():
                if know[e].get(k, 0) < v: know[e][k] = v
        waits.append(w)
        c = dict(know[e])
        c[done[0] if done is not None else e] = pos[i]
        clock.append(c)
    val, n, seen = {}, {}, {}
    for i, (e, fn, rd, wr, bk, done, name) in enumerate(ops):
        for j in waits[i]:
            s, v = ops[j][5] if ops[j][5] is not None else ("c" + ops[j][0], val[j])
            queue[e].wait_ge(T.sem[s], v)
            seen[s] = max(seen.get(s, 0), v)
        if fn is None: continue
        ins = fn()
        if done is not None:
            if ins is not None: ins.then_inc(T.sem[done[0]], 16)
        elif i in needed:
            n[e] = n.get(e, 0) + 1
            val[i] = n[e]
            ins.then_inc(T.sem["c" + e], 1)
    for s, v in final:
        if seen.get(s, 0) < v: g.wait_ge(T.sem[s], v)


def rank_program(g, core, T, topo):
    rank = T.rank_of(core)
    if rank is None:
        return
    N = len(T.cores)
    nxt, prv, opp = T.cores[(rank + 1) % N], T.cores[(rank - 1) % N], T.cores[(rank + 2) % N]
    ops, final, sent, now = [], [], [0], ["setup"]
    V, S, PE = g.vector, g.scalar, g.tensor

    def op(e, fn, rd, wr, bk=(), done=None):
        ops.append((e, fn, list(rd), list(wr), list(bk) + [k[0] for k in list(rd) + list(wr) if isinstance(k, tuple)], done, now[0]))

    def arrives(sem, count, keys):
        op("X", None, [], keys, done=(sem, count))
        final.append((sem, count))

    def hs(h, a=0): return slice(a + 16 * CUT[h], a + 16 * CUT[h + 1])
    def lst(buf, k, a=0, b=C): return buf[:, k * LS + a:k * LS + b]
    def nlst(k, a=0, b=C): return T.NL[:, k * C + a:k * C + b]
    def bank(i): return T["b%d" % i]
    def bh(i): return bank(i)[:, 0:16 * (CUT[i % 2 + 1] - CUT[i % 2])]
    def bl(i, n): return bank(i)[:, LB:LB + n]

    eq, mul, add, sub = ALU.is_equal, ALU.mult, ALU.add, ALU.subtract
    Sign, Relu, Ident, Tanh = ACT.Sign, ACT.Relu, ACT.Identity, ACT.Tanh

    def ts(out, in0, s1, s2, o0, o1, rd, wr):
        if s2 is None: op("V", lambda: V.tensor_scalar(out, in0, s1, None, o0), rd, wr)
        else: op("V", lambda: V.tensor_scalar(out, in0, s1, s2, o0, o1), rd, wr)

    def tt(out, a, b, o, rd, wr):
        op("V", lambda: V.tensor_tensor(out, a, b, o), rd, wr)

    def cp(out, a, rd, wr):
        op("V", lambda: V.tensor_copy(out, a), rd, wr)

    def act(out, a, f, rd, wr, bias=0.0, scale=1.0):
        op("S", lambda: S.activation(out, a, f, bias=bias, scale=scale), rd, wr)

    def scale_to(name, out, a, scale, rd, wr):
        if name in ONV: ts(out, a, scale, None, mul, None, rd, wr)
        else: act(out, a, Ident, rd, wr, scale=scale)

    def mm(key, out, m, rhs, start, stop, rd):
        op("P", lambda: PE.matmul(out, m, rhs, start, stop), rd + ([] if start else [key]), [key, (key[0], "group")])

    def turn(key, wt, n, src, lanes, rd):
        rows = (lanes.stop - lanes.start) // 16
        for i in range(16):
            mm(key, bank(key[0])[0:rows, i:16 * n:16], T[src][:, lanes.start + i:lanes.stop:16], wt, True, True, rd)

    def conv(key, wt, src, lanes, start, stop, rd):
        for i in range(16):
            mm(key, bl(key[0], (lanes.stop - lanes.start) // 16), T[wt][:, 15 - i:143 - i], T[src][:, lanes.start + i:lanes.stop:16],
               start and i == 0, stop and i == 15, rd + [wt])

    def fetch(name, key, at, rows, slot):
        scale_to(name, T.TT[0:rows, 128 * slot:128 * (slot + 1)], bank(key[0])[0:rows, at:at + 128], 1.0, [key], ["tt%d" % slot])

    def back(key, rows, slot, wt, start, stop):
        mm(key, bl(key[0], rows), T.TT[0:rows, 128 * slot:128 * (slot + 1)], T[wt][0:rows, 0:rows], start, stop, ["tt%d" % slot, wt])

    def uni(b, sel, buf, k, h, stop):
        mm((b, "h"), bh(b), T[sel][0:8, :], T[buf][0:8, hs(h, k * R)], True, stop, [sel, buf + ("1" if k else "0")])

    def load(e, name, out, src, key, after=()):
        q = g.sync if e == "Y" else g.scalar
        op(e, lambda: q.dma_start(out, src), after, [key], done=("ld_" + name, 16))
        final.append(("ld_" + name, 16))
    load("Y", "n0", T.n0i[:], T.n0[:], "n0i")
    load("S", "qd", T.Q0[:], T.qd[:], "Q0")
    load("Y", "pt", T.P[:], T.pt[:], "P")
    load("Y", "ud", T.UD[0:8, 0:R], T.ud[:, 0:R], "UD0")
    load("Y", "ua", T.UC[0:8, 0:R], T.ua[:, 0:R], "UC0")
    load("Y", "spot", T.spi[:], T.spot[:], "spi")
    load("Y", "ue", T.UD[0:8, R:], T.ud[:, R:], "UD1", ["P"])

    def spread(t):
        for x in range(16):
            op("Y", lambda x=x: g.sync.dma_start(T.UB[x:128:16, 2 * t * R:2 * (t + 1) * R], T.ua[:, (3 * t + 1) * R:3 * (t + 1) * R]),
               ["go%d" % (t - 1) if t else "P"], ["ub%d" % t] if x == 15 else [], done=("ub%d" % t, 256))
        final.append(("ub%d" % t, 256))

    def rest():
        load("Y", "nx", T.E[:], T.nx[:], "E", [LDKEY])
        load("Y", "ub", T.UC[0:8, 3 * R:], T.ua[:, 3 * R:], "UC1")
        load("Y", "vf", T.F[:], T.vf[:], "F")

    def iota(out, pat, cm, key):
        op("G", lambda: g.iota(out, pat, 0, cm, allow_small_or_imprecise_dtypes=True), [], [key])
    def col(k): return T.col[:, k:k + 1]
    G16, XC, R2, OM, G32, P16 = range(6)
    op("G", lambda: g.iota(T.pi[:, 0:1], [[0, 1]], 0, 1), [], ["pi0"])
    iota(T.um[:], [[1, 128]], -1, "um")
    iota(T.gm[:], [[16, 8], [0, 16]], 0, "gm")
    iota(T.col[0:8, P16:P16 + 1], [[0, 1]], 16, "p16")
    def numbers():
        op("G", lambda: g.iota(T.ji[:], [[1, 144]], -15, 0, allow_small_or_imprecise_dtypes=True), [], ["ji"])
    def numbers2():
        op("G", lambda: g.iota(T.ti[:], [[1, 32]], 0, -1), [], ["ti"])
        op("G", lambda: g.iota(T.tj[:], [[1, 128]], 0, -1), [], ["tj"])
    def scaled(*items):
        for name, src, scale in items:
            act(T[name][:], T[src][:, 0:T[name].shape[1]], Ident, [src], [name], scale=scale)
    def summed(b, names):
        for j, name in enumerate(names):
            mm((b, "h"), bank(b)[:, 0:128], T.mI[:], T[name][:], j == 0, j == len(names) - 1, ["mI", name])
    ts(T.pi[:, 1:2], T.pi[:, 0:1], 112, None, ALU.bitwise_and, None, ["pi0"], ["pi1"])
    ts(T.pi[:, 2:3], T.pi[:, 0:1], 15, None, ALU.bitwise_and, None, ["pi0"], ["pi2"])
    cp(T.col[:, G16:XC + 1], T.pi[:, 1:3], ["pi1", "pi2"], ["g16"])
    ts(T.mI[:], T.um[:], 0.0, None, eq, None, ["um"], ["mI"])

    def differences():
        ts(col(R2), col(XC), 15.0, -2.0, eq, mul, ["g16"], ["r2"])
        ts(T.t1[:], T.um[:], 1.0, -1.0, eq, mul, ["um"], ["t1"])
        ts(T.t2[:], T.um[:], -15.0, col(R2), eq, add, ["um", "r2"], ["t2"])
        summed(4, ["mI", "t1", "t2"])

    def blocks():
        ts(T.t0[:], T.um[:], 0.0, -0.5, ALU.is_ge, add, ["um"], ["t0"])
        ts(T.blk[:], T.gm[:], col(G16), None, eq, None, ["gm", "g16"], ["blk"])
        ts(T.sN[0:8, :], T.gm[0:8, :], T.col[0:8, P16:P16 + 1], -1.0, eq, mul, ["gm", "p16"], ["sN"])
        tt(T.t0[:], T.t0[:], T.blk[:], mul, ["t0", "blk"], ["t0"])
        ts(T.mN[:], T.t0[:], 0.0, -UNIT, ALU.is_gt, mul, ["t0"], ["mN"])

    def either():
        scaled(("t4", "mI", 2.0 ** 27), ("t5", "blk", -2.0 ** 26))
        summed(2, ["t4", "t5"])
    def either2():
        act(T.mA[:], bank(2)[:, 0:128], Ident, [(2, "h")], ["mA"])

    def verdicts():
        ts(col(OM), col(R2), -8.0, -1.0, mul, add, ["r2"], ["om"])
        ts(col(G32), col(G16), 16.0, None, add, None, ["g16"], ["g32"])
        if "cvk" not in TURN:
            ts(T.wK[:], T.ji[:], col(G16), col(OM), eq, mul, ["ji", "g16", "om"], ["wK"])
            ts(T.w0[:], T.ji[:], col(G32), col(OM), eq, mul, ["ji", "g32", "om"], ["w0"])
            tt(T.wK[:], T.wK[:], T.w0[:], add, ["wK", "w0"], ["wK"])
            return
        ts(T.gK[:, 8:16], T.gB[:], col(OM), None, mul, None, ["gB", "om"], ["gK1"])
        ts(T.gK[:, 16:24], T.gm[:, 0:128:16], col(G32), col(OM), eq, mul, ["gm", "g32", "om"], ["gK2"])
        tt(T.gK[:, 0:8], T.gK[:, 8:16], T.gK[:, 16:24], add, ["gK1", "gK2"], ["gK"])

    def onehot():
        ts(T.ti[:], T.ti[:], 15, None, ALU.bitwise_and, None, ["ti"], ["ti"])
        ts(T.OH[:], T.ti[:], 0.0, None, eq, None, ["ti"], ["OH"])

    def alternating():
        ts(T.tj[:], T.tj[:], 159, None, ALU.bitwise_and, None, ["tj"], ["tj"])
        ts(T.t1[:], T.tj[:], 0.0, None, eq, None, ["tj"], ["t1"])
        ts(T.t2[:], T.tj[:], 16.0, -1.0, eq, mul, ["tj"], ["t2"])
        tt(T.mT[:], T.t1[:], T.t2[:], add, ["t1", "t2"], ["mT"])

    def places():
        cp(T.sp1[:], T.spi[:], ["spi"], ["sp1"])
        cp(T.sph[:], T.sp1[:], ["sp1"], ["sph"])

    later = {
        "n0": lambda: cp(nlst(0), T.n0i[:], ["n0i"], ["NL0A", "NL0B"]),
        "m1": lambda: scaled(("mL", "mN", -256.0 / UNIT), ("mR", "mI", 128.0)),
        "m2": either, "m5": verdicts, "m6": onehot, "spc": places,
        "m3": lambda: scaled(("mO2", "t3", 2.0 ** 23), ("fB", "blk", -1.0), ("mW", "mN", -128.0 / UNIT)),
        "m4": lambda: scaled(("fL", "mN", 128.0 / UNIT), ("mF", "t0", 2.0 ** 26), ("wX", "wW", 16.0 / W)),
        "m7": alternating, "ld": rest, "m8": either2, "i1": numbers, "i2": numbers2, "c1": differences, "c2": blocks,
        "c3": lambda: tt(T.t3[:], T.blk[:], bank(4)[:, 0:128], mul, ["blk", (4, "h")], ["t3"]),
        "c4": lambda: cp(T.hI[:], T.mI[:], ["mI"], ["hI"]),
        "c5": lambda: ts(T.wW[:], T.ji[:], col(G16), float(W), eq, mul, ["ji", "g16"], ["wW"]),
        "c6": lambda: scaled(("mP", "mI", UNIT)), "c8": lambda: scaled(("mO1", "t3", 256.0)),
        "c7": lambda: act(T.sC[0:8, :], T.sN[0:8, :], Ident, ["sN"], ["sC"], scale=UNIT / 128),
        "qf": lambda: scale_to("qf", T.Q[:, 0:W], T.Q0[:], 1.0 / UNIT, ["Q0"], ["Q"]),
    }

    def share(src, dst, part, parts):
        es = topo.engines(src, dst)
        if parts > 1: es = [e for e in es if all(e in topo.engines(src, c) for c in T.cores if c != src)]
        if FEW: es = es[::len(es) // min(len(topo.engines(src, c)) for c in T.cores if c != src)]
        return es[part * len(es) // parts:(part + 1) * len(es) // parts]

    def send(items, rd):
        trs = []
        for j, (dst, out, srcs, sem) in enumerate(items):
            es = share(core, dst, j, len(items))
            rid, pid = topo.addr(dst, core)
            sent[0] += len(es)
            trs.append(RemoteDMATransfer(dst_ids=[DstId(rid=rid, pnc=pid)], dma_engine_mask=sum(1 << e for e in es), remote_sem=T.sem[sem],
                                         srcs=srcs, dsts=[out], alu_op=1 if len(srcs) > 1 else 0))
        def call():
            g.remote_dma_fused(trs, local_sem=T.sem.sent)
        op("G", call, rd, [], done=("sent", 0))

    def send_n(t):
        send([(nxt, lst(T.NI, t), [nlst(t)], "an%d" % t)], ["NL%dA" % t, "NL%dB" % t])
        arrives("an%d" % t, ne, ["NI%d" % t])

    def send_h(t):
        send([(prv if t == 2 else opp, lst(T.HI, t - 2), [nlst(t)], "ah%d" % t)], ["NL%dA" % t, "NL%dB" % t])
        arrives("ah%d" % t, len(share(nxt if t == 2 else opp, core, 0, 1)), ["HI%d" % (t - 2)])

    ne = len(share(prv, core, 0, 1))
    X, Y, Z, U = (0, 1), (2, 3), (4, 5), (6, 7)

    def steps(t):
        ni = "NI%d" % t
        last = t == TK - 1
        st = {}

        def half(h):
            k = "AB"[h]
            nl = "NL%d" % t + k
            sl, x, y, z, u = hs(h), X[h], Y[h], Z[h], U[h]
            xh, yh, zh, uh, xl, yl, ul = (x, "h"), (y, "h"), (z, "h"), (u, "h"), (x, "l"), (y, "l"), (u, "l")
            tl, c0, c1 = hs(h, t * R), CUT[h], CUT[h + 1]
            n, ls = c1 - c0, slice(c0, c1)
            qs, ps, fs, rs, mn = T.q1[:, tl], T.p1[:, tl], T.fo1[:, tl], T.rr[:, sl], T.mn[:, sl]
            kq, kp, kf, kd, ki, kr, km = ["%s%d%s" % (s, t, k) for s in ("q1", "p1", "fo1", "di", "fi")] + ["rr" + k, "mn" + k]
            own, inc = nlst(t, c0, c1), lst(T.NI, t, c0, c1)
            ub = [T.UB[:, hs(h, (2 * t + j) * R)] for j in (0, 1)]
            def lanes(name, land, srcs):
                ks = "AB" if name in WHOLE else k
                if ks[-1] != k: return
                a = slice(t * R, (t + 1) * R) if name in WHOLE else tl
                send([(nxt, T[land][:, a], [T[s][:, a] for s in srcs], "%s%s%d" % (name, k, t))],
                     ["%s%d%s" % (s, t, j) for s in srcs for j in ks])
                arrives("%s%s%d" % (name, k, t), ne, ["%si%d%s" % (name, t, j) for j in ks])
            def gq():
                if t == 0: scale_to("gq" + k, qs, T.Q0[:].indirect(own), -1.0 / UNIT, ["Q0", nl], [kq])
                else: scale_to("gq" + k, qs, T.Q[:, 0:W].indirect(own), -1.0, ["Q", nl], [kq])
            def rr():
                if "rr" + k in ONV: ts(rs, T.DI[:, tl], 0.0, 256.0 * UNIT, ALU.max, mul, [kd], [kr])
                else: act(rs, T.DI[:, tl], Relu, [kd], [kr], scale=256.0 * UNIT)
            def offsets(key, slot):
                mm(key, bl(key[0], n), T.hI[:], T.sph[:, t * C + c0:t * C + c1], True, False, ["hI", "sph"])
                back(key, n, slot, "wI", False, True)
            def x2(a, b):
                op("S", lambda: S.activation(T.Q[:].indirect(T.OF2[:, a:b]), T.p2[:, 16 * a:16 * b], Tanh), ["of2" + k, "p2"], ["Q"])
            d = {
                "a": lambda: uni(x, "sN", "UD", 2 * t, h, False),
                "c": lambda: uni(y, "sC", "UC", 3 * t, h, True),
                "gq": gq,
                "gp": lambda: scale_to("gp" + k, ps, T.P[:].indirect(own), 1.0 / UNIT, ["P", nl], [kp]),
                "tx": lambda: lanes("d", "DI", ["p1", "q1"]),
                "Lq": lambda: mm(xh, bh(x), T.mN[:], qs, False, True, ["mN", kq]),
                "Ip": lambda: mm(zh, bh(z), T.mP[:], ps, True, False, ["mP", kp]),
                "sg": lambda: act(T.s1[:, sl], bh(x), Sign, [xh], ["s1" + k], bias=-0.5),
                "cq": lambda: tt(T.cq[:, sl], qs, bh(y), mul, [kq, yh], ["cq" + k]),
                "pm": lambda: mm(zh, bh(z), T.mO1[:], T.s1[:, sl], False, True, ["mO1", "s1" + k]),
                "f": lambda: tt(fs, T.cq[:, sl], bh(z), ALU.is_lt, ["cq" + k, zh], [kf]),
                "tf": lambda: lanes("f", "FI", ["fo1"]),
                "cv": lambda: turn(uh, T.gB[:], 8, "fo1", tl, [kf, "gB"]),
                "ev": lambda: fetch("ev" + k, uh, 0, n, h),
                "cw": lambda: offsets(ul, h),
                "of": lambda: cp(T.OF1[:, ls], bl(u, n), [ul], ["of1" + k]),
                "x1": lambda: cp(T.Q[:].indirect(T.OF1[:, ls]), ps, ["of1" + k, kp], ["Q"]),
                "rr": rr,
                "b": lambda: uni(z, "sN", "UD", 2 * t + 1, h, False),
                "S": lambda: mm(yh, bh(y), T.blk[:], rs, True, True, ["blk", kr]),
                "Br": lambda: mm(uh, bh(u), T.blk[:], rs, True, False, ["blk", kr]),
                "qq": lambda: scale_to("qq" + k, T.q2[:, sl], T.Q[:, 0:W].indirect(inc), UNIT / 256, ["Q", ni],
                                       ["q2" + k] + (["go%d" % t] if h == 0 else [])),
                "sq": lambda: tt(bh(y), T.q2[:, sl], bh(y), mul, ["q2" + k, yh], [yh]),
                "L2": lambda: mm(zh, bh(z), T.mL[:], T.q2[:, sl], False, True, ["mL", "q2" + k]),
                "s2": lambda: act(T.s2[:, sl], bh(z), Sign, [zh], ["s2" + k], bias=-0.5),
                "I2": lambda: mm(xh, bh(x), T.mR[:], rs, True, False, ["mR", kr]),
                "A": lambda: mm(xh, bh(x), T.mA[:], T.FI[:, tl], False, False, ["mA", ki]),
                "p2": lambda: mm(xh, bh(x), T.mO2[:], T.s2[:, sl], False, True, ["mO2", "s2" + k]),
                "dq": lambda: tt(T.dq[:, sl], ub[0], bh(y), mul, ["ub%d" % t, yh], ["dq" + k]),
                "f2": lambda: tt(T.fo2[:, sl], T.dq[:, sl], bh(x), ALU.is_lt, ["dq" + k, xh], ["fo2" + k]),
                "mn": lambda: tt(mn, rs, bh(y), ALU.min, [kr, yh], [km]),
                "Bm": lambda: mm(uh, bh(u), T.fB[:], mn, False, True, ["fB", km]),
                "Lr": lambda: mm(zh, bh(z), T.mW[:], rs, True, False, ["mW", kr]),
                "Lm": lambda: mm(zh, bh(z), T.fL[:], mn, False, False, ["fL", km]),
                "ov": lambda: mm(zh, bh(z), T.mF[:], T.fo2[:, sl], False, True, ["mF", "fo2" + k]),
                "t": lambda: tt(T.th[:, sl], ub[1], bh(u), mul, ["ub%d" % t, uh], ["th" + k]),
                "sv": lambda: tt(T.sv[:, sl], T.th[:, sl], bh(z), ALU.is_lt, ["th" + k, zh], ["sv" + k]),
                "cvk": lambda: turn(yh, T.gK[:, 0:16], 16, "sv", sl, ["sv" + k, "gK"]),
                "ek": lambda: fetch("ek" + k, yh, 0, n, 2 + h),
                "ck": lambda: back(yl, n, 2 + h, "mI", True, True),
                "sgc": lambda: cp(T.SG[:, ls], bl(y, n), [yl], ["sg" + k]),
                "kb": lambda: fetch("kb" + k, yh, 128, n, 4 + h),
                "alt": lambda: back(ul, n, 4 + h, "mI", True, False),
                "eo": lambda: tt(T.eo[:, sl], T.OH[:].indirect(T.SG[:, ls]), T.ec[:, sl], mul, ["OH", "sg" + k, "ec"], ["eo" + k]),
                "cve": lambda: turn(zh, T.gB[:], 8, "eo", sl, ["eo" + k, "gB"]),
                "ee": lambda: fetch("ee" + k, zh, 0, n, 6 + h),
                "ce": lambda: back(ul, n, 6 + h, "xI", False, True),
                "nl": lambda: cp(nlst(t + 1, c0, c1), bl(u, n), [ul], ["NL%d" % (t + 1) + k]),
            }
            if last:
                d["yn"] = lambda: act(T.YN[:, t * C + c0:t * C + c1], bl(u, n), Ident, [ul], ["yn" + k])
                d["k"] = lambda: tt(T.hx[:, sl], T.F[:].indirect(inc), T.hh[:, sl], add, ["F", ni, "hh" + k], ["hx" + k])
                d["tk"] = lambda: act(T.hh[:, sl], T.hx[:, sl], Tanh, ["hx" + k], ["hh" + k])
            else:
                mid = c0 + n // 4 * 2
                d["oc"] = lambda: turn(xh, T.gB[:], 8, "fo2", sl, ["fo2" + k, "gB"])
                d["oe"] = lambda: fetch("oe" + k, xh, 0, n, 8 + h)
                d["ow"] = lambda: offsets(xl, 8 + h)
                d["og"] = lambda: cp(T.OF2[:, ls], bl(x, n), [xl], ["of2" + k])
                d["x2"] = lambda: x2(c0, mid)
                d["y2"] = lambda: x2(mid, c1)
            def place(key):
                mm(key, bl(key[0], n), T.hI[:], T.sph[:, t * C + c0:t * C + c1], True, False, ["hI", "sph"])
            if "cv" not in TURN:
                d["cv"] = lambda: place(ul)
                d["cw"] = lambda: conv(ul, "wW", "fo1", tl, False, True, [kf])
                del d["ev"]
            if "oc" not in TURN and not last:
                d["oc"] = lambda: place(xl)
                d["ow"] = lambda: conv(xl, "wW", "fo2", sl, False, True, ["fo2" + k])
                del d["oe"]
            if "cve" not in TURN:
                d["ce"] = lambda: conv(ul, "wX", "eo", sl, False, True, ["eo" + k])
                del d["cve"], d["ee"]
            if "cvk" not in TURN:
                d["ck"] = lambda: conv(yl, "wK", "sv", sl, True, True, ["sv" + k])
                d["kb"] = lambda: scale_to("kb" + k, T.KB[:, ls], bl(y, n), 1.0, [yl], ["kb" + k])
                d["alt"] = lambda: mm(ul, bl(u, n), T.mT[:], T.KB[:, ls], True, False, ["mT", "kb" + k])
                del d["cvk"], d["ek"]
            if WIDE and not last:
                if h == 0: del d["oc"], d["ow"], d["og"]
                else:
                    d["oc"] = lambda: mm(xl, bl(x, C), T.hI[:], T.sph[:, t * C:(t + 1) * C], True, False, ["hI", "sph"])
                    d["ow"] = lambda: conv(xl, "wW", "fo2", slice(0, R), False, True, ["fo2A", "fo2B"])
                    d["og"] = lambda: cp(T.OF2[:], bl(x, C), [xl], ["of2A", "of2B"])
            if "k" in BOTH:
                if h == 0: del d["ck"], d["sgc"], d["kb"]
                else:
                    d["ck"] = lambda: conv(yl, "wK", "sv", slice(0, R), True, True, ["svA", "svB"])
                    d["sgc"] = lambda: cp(T.SG[:], bl(y, C), [yl], ["sgA", "sgB"])
                    d["kb"] = lambda: scale_to("kb" + k, T.KB[:], bl(y, C), 1.0, [yl], ["kbA", "kbB"])
            if "e" in BOTH:
                if h == 0:
                    del d["alt"], d["ce"], d["nl"]
                    if last: del d["yn"]
                else:
                    d["alt"] = lambda: mm(ul, bl(u, C), T.mT[:], T.KB[:], True, False, ["mT", "kbA", "kbB"])
                    d["ce"] = lambda: conv(ul, "wX", "eo", slice(0, R), False, True, ["eoA", "eoB"])
                    d["nl"] = lambda: cp(nlst(t + 1), bl(u, C), [ul], ["NL%dA" % (t + 1), "NL%dB" % (t + 1)])
                    if last: d["yn"] = lambda: act(T.YN[:, t * C:(t + 1) * C], bl(u, C), Ident, [ul], ["ynA", "ynB"])
            if not last and k not in SPLIT:
                d["x2"] = lambda: x2(c0, c1)
                del d["y2"]
            for name in d:
                st[name + k] = d[name]
        half(0)
        half(1)

        hh, hx = ["hhA", "hhB"], ["hxA", "hxB"]
        st.update({
            "sn": lambda: send_n(t), "bc": lambda: spread(t),
            "ecg": lambda: scale_to("ecg", T.ec[:], T.E[:].indirect(lst(T.NI, t)), 1.0, ["E", ni], ["ec"]),
        })
        if not last:
            st["g2"] = lambda: scale_to("g2", T.p2[:], T.P[:].indirect(lst(T.NI, t)), 1.0 / UNIT, ["P", ni], ["p2"])
        if t == 1:
            st["th"] = lambda: act(T.hh[:], T.F[:].indirect(nlst(1)), Tanh, ["F", "NL1A", "NL1B"], hh)
        if t in (2, 3):
            st["sh"] = lambda: send_h(t)
            st["hg"] = lambda: act(T.hx[:], T.F[:].indirect(lst(T.HI, t - 2)), Ident, ["F", "HI%d" % (t - 2)], hx)
            st["hd"] = lambda: op("G", lambda: g.dma_start(T.hh[:], T.hx[:], accum_op=add), hx + hh, hh, done=("hd%d" % t, 16))
        if t in (3, 4):
            st["th"] = lambda: act(T.hh[:], T.hh[:], Tanh, hh, hh)
        if last:
            st["yn"] = lambda: cp(T.YN[:, 0:t * C], T.NL[:, C:TK * C], ["NL%d%s" % (j, k) for j in range(1, TK) for k in "AB"], ["yn"])
        return st

    def out_h(k, a, b):
        sl = slice(16 * a, 16 * b)
        tt(T.hx[:, sl], T.F[:].indirect(nlst(TK, a, b)), T.hh[:, sl], add, ["F", "NL%d" % TK + k, "hh" + k], ["hz%d" % a])
        act(T.ho[:, sl], T.hx[:, sl], Tanh, ["hz%d" % a], ["ho%d" % a])
        op("Y", lambda: g.sync.dma_start(T.yh[:, sl], T.ho[:, sl]), ["ho%d" % a], [], done=("stored", 16))

    def out_n():
        op("S", lambda: g.scalar.dma_start(T.yn[:], T.YN[:]), ["yn", "ynA", "ynB"], [], done=("stored", 16))

    every = [steps(t) for t in range(TK)] + [{
        "gqA": lambda: out_h("A", 0, TAIL[0]), "gpA": lambda: out_h("A", TAIL[0], CUT[1]),
        "gqB": lambda: out_h("B", CUT[1], TAIL[1]), "gpB": lambda: out_h("B", TAIL[1], C), "sn": out_n}]
    every[0].update(later)
    for t, names in [(0, FIRST)] + [(t, ORDER) for t in range(TK - 1)] + [(TK - 1, LAST)]:
        for name in names:
            u = t + 1 if name[0] == "+" else t
            now[0] = name.lstrip("+") + str(u)
            if name.lstrip("+") in every[u]: every[u][name.lstrip("+")]()
    final.append(("stored", 16 * 5))
    final.append(("sent", sent[0]))
    emit(g, T, ops, final)
